import numpy as np
import ml_dtypes


def mxq(x, axis, fmt="e4m3"):
    dtype, down = {"e4m3": (ml_dtypes.float8_e4m3fn, 7), "e5m2": (ml_dtypes.float8_e5m2, 14)}[fmt]
    v = np.moveaxis(np.asarray(x, np.float32).astype(ml_dtypes.bfloat16).astype(np.float64), axis, -1)
    blocks = v.reshape(v.shape[:-1] + (-1, 32))
    amax = np.abs(blocks).max(-1, keepdims=True)
    byte = np.maximum(np.where(amax > 0, np.frexp(amax)[1] - 1 + 127, 0) - down, 1)
    scale = np.exp2(byte - 127.0)
    codes = (blocks / scale).astype(np.float32).astype(dtype).astype(np.float64)
    return np.moveaxis((codes * scale).reshape(v.shape), -1, axis)


WIDE = False


def mx_kscale(k):
    if not WIDE:
        return np.ones(k)
    levels = np.array([24, -24, 12, -12, 0])
    if k % 512:
        return np.exp2(np.random.permutation(np.resize(levels, k // 32))).repeat(32)
    a = np.empty((k // 512, 16))
    for p in range(k // 512):
        a[p, :8] = np.random.permutation(np.resize(levels, 8))
        for g in range(8):
            far = levels[np.abs(levels - a[p, g]) >= 10]
            a[p, g + 8] = far[np.random.randint(len(far))]
    return np.exp2(a.ravel()).repeat(32)


def f64(x):
    return np.asarray(x).astype(np.float64)


def striped(idx):
    return np.tile(idx.reshape(-1, 16).T, (8, 1)).astype(np.uint16)


def unstriped(offs):
    return offs[:16].T.reshape(-1).astype(np.int64)


E2M1 = np.array([0.0, 0.5, 1.0, 1.5, 2.0, 3.0, 4.0, 6.0, -0.0, -0.5, -1.0, -1.5, -2.0, -3.0, -4.0, -6.0])


def pack_weight(w, fmt):
    k, n = w.shape
    w = f64(np.asarray(w, np.float32).astype(ml_dtypes.bfloat16)).reshape(k // 32, 32, n)
    amax = np.abs(w).max(1)
    if fmt == "e4m3":
        byte = np.frexp(amax)[1] - 1 + 127 - 7
    else:
        mant, ex = np.frexp(amax / 6.0)
        byte = np.where(mant > 0.5, ex, ex - 1) + 127
    byte = np.clip(np.where(amax > 0, byte, 1), 1, 254)
    scaled = (w * np.exp2(127.0 - byte)[:, None, :]).reshape(k, n).astype(np.float32)
    by_word = np.ascontiguousarray(scaled.reshape(k // 512, 128, 4, n).transpose(0, 1, 3, 2))
    if fmt == "e4m3":
        words = by_word.astype(ml_dtypes.float8_e4m3fn).view(np.uint8)
    else:
        c = by_word.astype(ml_dtypes.float4_e2m1fn).view(np.uint8) & 0xF
        words = (c[..., 0::2] | (c[..., 1::2] << 4)).reshape(k // 512, 128, 2 * n)
    return np.ascontiguousarray(words), np.ascontiguousarray(byte.astype(np.uint8).reshape(k // 512, 16, n))


def unpack_weight(words, scales, fmt):
    g, _, n = scales.shape
    words = np.ascontiguousarray(words).reshape(g, 128, n, -1)
    if fmt == "e4m3":
        vals = words.view(ml_dtypes.float8_e4m3fn).astype(np.float64)
    else:
        nib = np.empty((g, 128, n, 4), np.uint8)
        nib[..., 0::2] = words & 0xF
        nib[..., 1::2] = words >> 4
        vals = E2M1[nib]
    vals = vals * np.repeat(np.exp2(scales.astype(np.float64) - 127.0), 8, axis=1)[..., None]
    return vals.transpose(0, 1, 3, 2).reshape(g * 512, n)


def pack_table4(v):
    words, scales = pack_weight(v, "e2m1")
    g, t = words.shape[0] // 2, v.shape[1]
    return np.ascontiguousarray(words.reshape(g, 2, 128, t, 2).transpose(0, 2, 3, 1, 4).reshape(g, 128, t, 4)), scales


def unpack_table4(words, scales):
    g, _, t, _ = words.shape
    return unpack_weight(words.reshape(g, 128, t, 2, 2).transpose(0, 3, 1, 2, 4).reshape(2 * g, 128, 2 * t), scales, "e2m1")


def silu(f):
    return f / (1.0 + np.exp(-np.maximum(f, -700.0)))


def sigm(f):
    return 1.0 / (1.0 + np.exp(-np.maximum(f, -700.0)))


K, N, T, J = 1024, 512, 1024, 512


def setup_inputs():
    n = np.random.standard_normal
    s = mx_kscale(K)[:, None]
    wh = n((K, N)) / np.sqrt(K) / s
    p_tab = pack_table4(n((K, T)) * s)
    p_wg = pack_weight(n((K, N)) / np.sqrt(K) / s, "e4m3")
    p_wh4 = pack_weight(wh[512:], "e2m1")
    return {
        "tab_words": p_tab[0],
        "tab_scales": p_tab[1],
        "wg_words": p_wg[0],
        "wg_scales": p_wg[1],
        "wh8": (wh[:512]).astype(np.float32),
        "wh4_words": p_wh4[0],
        "wh4_scales": p_wh4[1],
        "bg": (0.3 * n(N) - 1.0).astype(np.float32),
        "rT": (n((N, T))).astype(np.float32),
        "offs": striped(np.random.permutation(T)[:J]),
    }


def reference(tab_words, tab_scales, wg_words, wg_scales, wh8, wh4_words, wh4_scales, bg, rT, offs):
    idx = unstriped(offs)
    tab_ = unpack_table4(tab_words, tab_scales)[:, idx]
    wg_ = unpack_weight(wg_words, wg_scales, "e4m3")
    wh8_ = mxq(f64(wh8), 0, "e4m3")
    wh4_ = unpack_weight(wh4_words, wh4_scales, "e2m1")
    ga = wg_.T @ tab_
    gate = sigm(ga + f64(bg)[:, None])
    ha = wh8_.T @ tab_[:512] + wh4_.T @ tab_[512:]
    return f64(rT)[:, idx] + gate * (silu(ha) - f64(rT)[:, idx])

@@ -1,0 +1,216 @@
+from contextlib import ExitStack
+
+import concourse.mybir as mybir
+
+K, N, T, J = 1024, 512, 1024, 512
+FLOPS = 2 * 2 * K * N * J
+
+F32 = mybir.dt.float32
+BF16 = mybir.dt.bfloat16
+I32 = mybir.dt.int32
+U32 = mybir.dt.uint32
+U16 = mybir.dt.uint16
+U8 = mybir.dt.uint8
+FP8X4 = mybir.dt.float8_e4m3fn_x4
+FP4X4 = mybir.dt.float4_e2m1fn_x4
+ACT = mybir.ActivationFunctionType
+ALU = mybir.AluOpType
+
+P = 128
+HALF = J // 2
+NARROW = 128
+
+
+def tile_list_hwayt_qf_silu_kernel(
+    tc, tab_words, tab_scales, wg_words, wg_scales, wh8, wh4_words, wh4_scales, bg, rT, offs, out
+):
+    nc = tc.nc
+    with ExitStack() as ctx:
+        sb = ctx.enter_context(tc.tile_pool(name="sb", bufs=1))
+        ps = ctx.enter_context(tc.psum_pool(name="ps", bufs=1))
+
+        offsets = sb.tile([P, J // 16], U16, name="offsets")
+        tab_sc = sb.tile([P, 2, T // 4], I32, name="tab_sc", align_bytes=64)
+        tab_w = sb.tile([P, T], I32, name="tab_w", align_bytes=64)
+        wg_sc = sb.tile([P, 2, N // 4], I32, name="wg_sc", align_bytes=64)
+        wg_w = sb.tile([P, 2, N], I32, name="wg_w", align_bytes=64)
+        wh4_sc = sb.tile([P, N // 4], I32, name="wh4_sc", align_bytes=64)
+        wh4_w = sb.tile([P, N // 2], I32, name="wh4_w", align_bytes=64)
+        bias = sb.tile([P, 4], F32, name="bias")
+        half_bias = sb.tile([P, 4], F32, name="half_bias")
+        zero_in = sb.tile([P, 1], F32, name="zero_in")
+        zero = sb.tile([P, 1], F32, name="zero")
+        raw = [sb.tile([P, 4, N // 2], F32, name="raw%d" % u, align_bytes=64) for u in range(2)]
+        grouped = [sb.tile([P, N // 2, 4], BF16, name="grouped%d" % u, align_bytes=64) for u in range(2)]
+        wh8_w = [sb.tile([P, N // 2], U32, name="wh8_w%d" % u, align_bytes=64) for u in range(2)]
+        wh8_sc = [sb.tile([P, N // 2], U8, name="wh8_sc%d" % u, align_bytes=64) for u in range(2)]
+        rec = [sb.tile([P, T], F32, name="rec%d" % c, align_bytes=64) for c in range(4)]
+        got_w = sb.tile([P, J], U32, name="got_w", align_bytes=64)
+        got_sc = sb.tile([P, 2, J], U8, name="got_sc", align_bytes=64)
+        item_w = sb.tile([P, 2, J], U16, name="item_w", align_bytes=64)
+        th = [sb.tile([P, J], F32, name="th%d" % c) for c in range(4)]
+        carry = [sb.tile([P, J], F32, name="carry%d" % c) for c in range(4)]
+        act = [sb.tile([P, J], F32, name="act%d" % c) for c in range(4)]
+        kept = [sb.tile([P, J], F32, name="kept%d" % c) for c in range(4)]
+        made = [sb.tile([P, J], F32, name="made%d" % c) for c in range(4)]
+        res = [sb.tile([P, J], F32, name="res%d" % c) for c in range(4)]
+
+        nc.vector.memset(tab_sc[:], 0)
+        nc.gpsimd.memset(zero_in[:], 0.0)
+        nc.scalar.activation(out=zero[:], in_=zero_in[:], func=ACT.Silu)
+        nc.vector.memset(wg_sc[:], 0)
+        nc.vector.memset(wh4_sc[:], 0)
+
+        def load_scale_rows(queue, plane, rows):
+            for q in range(4):
+                queue.dma_start(
+                    out=plane[32 * q : 32 * q + 4],
+                    in_=rows[:, 4 * q : 4 * q + 4, :].rearrange("a r t -> r a t").bitcast(I32),
+                )
+
+        def load_wh8(u):
+            nc.sync.dma_start(
+                out=raw[u][:],
+                in_=wh8[:, u * 256 : (u + 1) * 256].rearrange("(p i) n -> p i n", i=4),
+            )
+
+        def load_rec(c):
+            nc.sync.dma_start(out=rec[c][:], in_=rT[c * P : (c + 1) * P, :])
+
+        nc.sync.dma_start(offsets[:], offs)
+        with nc.allow_non_contiguous_dma(reason="one bias value to a partition"):
+            nc.gpsimd.dma_start(out=bias[:], in_=bg.rearrange("(c p) -> p c", p=P))
+        nc.sync.dma_start(out=tab_w[:], in_=tab_words[0].rearrange("p t b -> p (t b)").bitcast(I32))
+        nc.sync.dma_start(out=wh4_w[:], in_=wh4_words[0].bitcast(I32))
+        load_scale_rows(nc.sync, tab_sc, tab_scales)
+        nc.sync.dma_start(out=wg_w[:], in_=wg_words.rearrange("a p n i -> p a (n i)").bitcast(I32))
+        load_wh8(0)
+        load_scale_rows(nc.sync, wg_sc, wg_scales)
+        load_rec(0)
+        for q in range(4):
+            nc.sync.dma_start(
+                out=wh4_sc[32 * q : 32 * q + 4, :], in_=wh4_scales[0, 4 * q : 4 * q + 4, :].bitcast(I32)
+            )
+        load_rec(1)
+        load_wh8(1)
+        load_rec(2)
+        load_rec(3)
+
+        nc.scalar.activation(out=half_bias[:], in_=bias[:], func=ACT.Copy, scale=0.5)
+
+        def cols(h):
+            return slice(h * HALF, (h + 1) * HALF)
+
+        def offs_of(h):
+            return offsets[:, h * (HALF // 16) : (h + 1) * (HALF // 16)]
+
+        def gather_scales(a, h):
+            nc.vector.tensor_copy(
+                out=got_sc[:, a, cols(h)], in_=tab_sc[:, a, :].bitcast(U8).indirect(offs_of(h))
+            )
+
+        def round_wh8(u):
+            nc.scalar.copy(
+                out=grouped[u][:].rearrange("p (c m) i -> p c i m", m=4),
+                in_=raw[u][:].rearrange("p i (c m) -> p c i m", m=4),
+            )
+
+        def quantize_wh8(u):
+            nc.vector.quantize_mx(
+                out=wh8_w[u][:].bitcast(FP8X4),
+                scales=wh8_sc[u][:],
+                in_=grouped[u][:].rearrange("p n i -> p (n i)"),
+            )
+
+        def gate(c, j0, width, step, tag):
+            acc = ps.tile([P, width], F32, name="ga", tag=tag)
+            for s in range(0, width, step):
+                js = slice(j0 + s, j0 + s + step)
+                for a in range(2):
+                    nc.tensor.matmul_mx(
+                        out=acc[:, s : s + step],
+                        lhsT=wg_w[:, a, c * P : (c + 1) * P].bitcast(FP8X4),
+                        lhsT_scale=wg_sc[:, a, c * 32 : (c + 1) * 32].bitcast(U8),
+                        rhs=item_w[:, a, js].bitcast(FP4X4),
+                        rhs_scale=got_sc[:, a, js],
+                        start=(a == 0),
+                        stop=(a == 1),
+                    )
+            js = slice(j0, j0 + width)
+            nc.scalar.activation(
+                out=th[c][:, js], in_=acc[:], func=ACT.Tanh, bias=half_bias[:, c : c + 1], scale=0.5
+            )
+            nc.scalar.activation(out=carry[c][:, js], in_=th[c][:, js], func=ACT.Copy, bias=0.5, scale=-0.5)
+
+        def hidden(c, tag):
+            acc = ps.tile([P, J], F32, name="ha", tag=tag)
+            u, m = divmod(c, 2)
+            nc.tensor.matmul_mx(
+                out=acc[:],
+                lhsT=wh4_w[:, c * 64 : (c + 1) * 64].bitcast(FP4X4),
+                lhsT_scale=wh4_sc[:, c * 32 : (c + 1) * 32].bitcast(U8),
+                rhs=item_w[:, 1, :].bitcast(FP4X4),
+                rhs_scale=got_sc[:, 1, :],
+                start=True,
+                stop=False,
+            )
+            nc.tensor.matmul_mx(
+                out=acc[:],
+                lhsT=wh8_w[u][:, m * P : (m + 1) * P].bitcast(FP8X4),
+                lhsT_scale=wh8_sc[u][:, m * P : (m + 1) * P],
+                rhs=item_w[:, 0, :].bitcast(FP4X4),
+                rhs_scale=got_sc[:, 0, :],
+                start=False,
+                stop=True,
+            )
+            nc.scalar.activation(out=act[c][:], in_=acc[:], func=ACT.Silu, bias=zero[:])
+
+        def keep(c, c0, c1):
+            js = slice(16 * c0, 16 * c1)
+            nc.vector.tensor_tensor(
+                out=kept[c][:, js], in0=rec[c][:].indirect(offsets[:, c0:c1]), in1=carry[c][:, js], op=ALU.mult
+            )
+
+        def make(c):
+            nc.vector.scalar_tensor_tensor(
+                out=made[c][:], in0=carry[c][:], scalar=1.0, in1=act[c][:], op0=ALU.subtract, op1=ALU.mult
+            )
+
+        def finish(c):
+            nc.vector.tensor_tensor(out=res[c][:], in0=kept[c][:], in1=made[c][:], op=ALU.subtract)
+            nc.sync.dma_start(out=out[c * P : (c + 1) * P, :], in_=res[c][:])
+
+        nc.vector.tensor_copy(out=got_w[:], in_=tab_w[:].bitcast(U32).indirect(offsets[:]))
+        gather_scales(0, 0)
+        nc.vector.tensor_copy(out=item_w[:], in_=got_w[:].bitcast(U16).rearrange("p (j d) -> p d j", d=2))
+        gather_scales(1, 0)
+        round_wh8(0)
+        gate(0, 0, HALF, NARROW, "b0")
+        gate(1, 0, HALF, NARROW, "b1")
+        gather_scales(0, 1)
+        gather_scales(1, 1)
+        quantize_wh8(0)
+        gate(0, HALF, HALF, NARROW, "b2")
+        gate(1, HALF, HALF, NARROW, "b3")
+        hidden(0, "b4")
+        hidden(1, "b5")
+        keep(0, 0, 16)
+        keep(1, 0, 16)
+        keep(0, 16, 32)
+        keep(1, 16, 32)
+        round_wh8(1)
+        gate(2, 0, J, J, "b6")
+        gate(3, 0, J, J, "b7")
+        make(0)
+        make(1)
+        quantize_wh8(1)
+        hidden(2, "b0")
+        hidden(3, "b1")
+        finish(0)
+        finish(1)
+        keep(2, 0, 32)
+        make(2)
+        keep(3, 0, 32)
+        finish(2)
+        make(3)
+        finish(3)

@@ -37,7 +37,7 @@ def tile_list_hwayt_qf_silu_kernel(
         wh4_sc = sb.tile([P, N // 4], I32, name="wh4_sc", align_bytes=64)
         wh4_w = sb.tile([P, N // 2], I32, name="wh4_w", align_bytes=64)
         bias = sb.tile([P, 4], F32, name="bias")
-        half_bias = sb.tile([P, 4], F32, name="half_bias")
+        neg_bias = sb.tile([P, 4], F32, name="neg_bias")
         zero_in = sb.tile([P, 1], F32, name="zero_in")
         zero = sb.tile([P, 1], F32, name="zero")
         raw = [sb.tile([P, 4, N // 2], F32, name="raw%d" % u, align_bytes=64) for u in range(2)]
@@ -48,7 +48,6 @@ def tile_list_hwayt_qf_silu_kernel(
         got_w = sb.tile([P, J], U32, name="got_w", align_bytes=64)
         got_sc = sb.tile([P, 2, J], U8, name="got_sc", align_bytes=64)
         item_w = sb.tile([P, 2, J], U16, name="item_w", align_bytes=64)
-        th = [sb.tile([P, J], F32, name="th%d" % c) for c in range(4)]
         carry = [sb.tile([P, J], F32, name="carry%d" % c) for c in range(4)]
         act = [sb.tile([P, J], F32, name="act%d" % c) for c in range(4)]
         kept = [sb.tile([P, J], F32, name="kept%d" % c) for c in range(4)]
@@ -56,8 +55,7 @@ def tile_list_hwayt_qf_silu_kernel(
         res = [sb.tile([P, J], F32, name="res%d" % c) for c in range(4)]
 
         nc.vector.memset(tab_sc[:], 0)
-        nc.gpsimd.memset(zero_in[:], 0.0)
-        nc.scalar.activation(out=zero[:], in_=zero_in[:], func=ACT.Silu)
+        nc.vector.memset(zero_in[:], -200.0)
         nc.vector.memset(wg_sc[:], 0)
         nc.vector.memset(wh4_sc[:], 0)
 
@@ -79,24 +77,25 @@ def tile_list_hwayt_qf_silu_kernel(
 
         nc.sync.dma_start(offsets[:], offs)
         with nc.allow_non_contiguous_dma(reason="one bias value to a partition"):
-            nc.gpsimd.dma_start(out=bias[:], in_=bg.rearrange("(c p) -> p c", p=P))
+            nc.scalar.dma_start(out=bias[:], in_=bg.rearrange("(c p) -> p c", p=P))
         nc.sync.dma_start(out=tab_w[:], in_=tab_words[0].rearrange("p t b -> p (t b)").bitcast(I32))
-        nc.sync.dma_start(out=wh4_w[:], in_=wh4_words[0].bitcast(I32))
         load_scale_rows(nc.sync, tab_sc, tab_scales)
-        nc.sync.dma_start(out=wg_w[:], in_=wg_words.rearrange("a p n i -> p a (n i)").bitcast(I32))
+        nc.scalar.activation(out=zero[:], in_=zero_in[:], func=ACT.Sigmoid)
         load_wh8(0)
+        load_wh8(1)
         load_scale_rows(nc.sync, wg_sc, wg_scales)
+        nc.sync.dma_start(out=wg_w[:], in_=wg_words.rearrange("a p n i -> p a (n i)").bitcast(I32))
         load_rec(0)
+        load_rec(1)
+        load_rec(2)
+        nc.sync.dma_start(out=wh4_w[:], in_=wh4_words[0].bitcast(I32))
         for q in range(4):
             nc.sync.dma_start(
                 out=wh4_sc[32 * q : 32 * q + 4, :], in_=wh4_scales[0, 4 * q : 4 * q + 4, :].bitcast(I32)
             )
-        load_rec(1)
-        load_wh8(1)
-        load_rec(2)
         load_rec(3)
 
-        nc.scalar.activation(out=half_bias[:], in_=bias[:], func=ACT.Copy, scale=0.5)
+        nc.scalar.activation(out=neg_bias[:], in_=bias[:], func=ACT.Identity, scale=-1.0, bias=zero[:])
 
         def cols(h):
             return slice(h * HALF, (h + 1) * HALF)
@@ -138,9 +137,8 @@ def tile_list_hwayt_qf_silu_kernel(
                     )
             js = slice(j0, j0 + width)
             nc.scalar.activation(
-                out=th[c][:, js], in_=acc[:], func=ACT.Tanh, bias=half_bias[:, c : c + 1], scale=0.5
+                out=carry[c][:, js], in_=acc[:], func=ACT.Sigmoid, bias=neg_bias[:, c : c + 1], scale=-1.0
             )
-            nc.scalar.activation(out=carry[c][:, js], in_=th[c][:, js], func=ACT.Copy, bias=0.5, scale=-0.5)
 
         def hidden(c, tag):
             acc = ps.tile([P, J], F32, name="ha", tag=tag)
@@ -163,7 +161,7 @@ def tile_list_hwayt_qf_silu_kernel(
                 start=False,
                 stop=True,
             )
-            nc.scalar.activation(out=act[c][:], in_=acc[:], func=ACT.Silu, bias=zero[:])
+            nc.scalar.activation(out=act[c][:], in_=acc[:], func=ACT.Silu)
 
         def keep(c, c0, c1):
             js = slice(16 * c0, 16 * c1)
@@ -176,41 +174,42 @@ def tile_list_hwayt_qf_silu_kernel(
                 out=made[c][:], in0=carry[c][:], scalar=1.0, in1=act[c][:], op0=ALU.subtract, op1=ALU.mult
             )
 
-        def finish(c):
-            nc.vector.tensor_tensor(out=res[c][:], in0=kept[c][:], in1=made[c][:], op=ALU.subtract)
-            nc.sync.dma_start(out=out[c * P : (c + 1) * P, :], in_=res[c][:])
+        def finish(c, js, queue):
+            nc.vector.tensor_tensor(out=res[c][:, js], in0=kept[c][:, js], in1=made[c][:, js], op=ALU.subtract)
+            queue.dma_start(out=out[c * P : (c + 1) * P, js], in_=res[c][:, js])
 
         nc.vector.tensor_copy(out=got_w[:], in_=tab_w[:].bitcast(U32).indirect(offsets[:]))
-        gather_scales(0, 0)
         nc.vector.tensor_copy(out=item_w[:], in_=got_w[:].bitcast(U16).rearrange("p (j d) -> p d j", d=2))
+        gather_scales(0, 0)
         gather_scales(1, 0)
         round_wh8(0)
+        round_wh8(1)
         gate(0, 0, HALF, NARROW, "b0")
         gate(1, 0, HALF, NARROW, "b1")
         gather_scales(0, 1)
         gather_scales(1, 1)
         quantize_wh8(0)
+        quantize_wh8(1)
         gate(0, HALF, HALF, NARROW, "b2")
         gate(1, HALF, HALF, NARROW, "b3")
-        hidden(0, "b4")
-        hidden(1, "b5")
+        gate(2, 0, J, J, "b4")
+        gate(3, 0, J, J, "b5")
         keep(0, 0, 16)
         keep(1, 0, 16)
         keep(0, 16, 32)
         keep(1, 16, 32)
-        round_wh8(1)
-        gate(2, 0, J, J, "b6")
-        gate(3, 0, J, J, "b7")
-        make(0)
-        make(1)
-        quantize_wh8(1)
+        keep(2, 0, 32)
+        keep(3, 0, 32)
+        hidden(0, "b6")
+        hidden(1, "b7")
         hidden(2, "b0")
         hidden(3, "b1")
-        finish(0)
-        finish(1)
-        keep(2, 0, 32)
+        make(0)
+        make(1)
+        finish(0, slice(0, J), nc.sync)
         make(2)
-        keep(3, 0, 32)
-        finish(2)
+        finish(1, slice(0, J), nc.sync)
         make(3)
-        finish(3)
+        finish(2, slice(0, J), nc.sync)
+        finish(3, cols(0), nc.sync)
+        finish(3, cols(1), nc.scalar)

@@ -1,6 +1,7 @@
 from contextlib import ExitStack
 
 import concourse.mybir as mybir
+from concourse.masks import make_identity
 
 K, N, T, J = 1024, 512, 1024, 512
 FLOPS = 2 * 2 * K * N * J
@@ -36,7 +37,8 @@ def tile_list_hwayt_qf_silu_kernel(
         wg_w = sb.tile([P, 2, N], I32, name="wg_w", align_bytes=64)
         wh4_sc = sb.tile([P, N // 4], I32, name="wh4_sc", align_bytes=64)
         wh4_w = sb.tile([P, N // 2], I32, name="wh4_w", align_bytes=64)
-        bias = sb.tile([P, 4], F32, name="bias")
+        bias_rows = sb.tile([P, P], F32, name="bias_rows")
+        ident = sb.tile([P, P], F32, name="ident")
         neg_bias = sb.tile([P, 4], F32, name="neg_bias")
         zero_in = sb.tile([P, 1], F32, name="zero_in")
         zero = sb.tile([P, 1], F32, name="zero")
@@ -55,7 +57,9 @@ def tile_list_hwayt_qf_silu_kernel(
         res = [sb.tile([P, J], F32, name="res%d" % c) for c in range(4)]
 
         nc.vector.memset(tab_sc[:], 0)
-        nc.vector.memset(zero_in[:], -200.0)
+        nc.gpsimd.memset(bias_rows[:], 0.0)
+        nc.gpsimd.memset(zero_in[:], -200.0)
+        make_identity(nc, ident[:])
         nc.vector.memset(wg_sc[:], 0)
         nc.vector.memset(wh4_sc[:], 0)
 
@@ -76,8 +80,7 @@ def tile_list_hwayt_qf_silu_kernel(
             nc.sync.dma_start(out=rec[c][:], in_=rT[c * P : (c + 1) * P, :])
 
         nc.sync.dma_start(offsets[:], offs)
-        with nc.allow_non_contiguous_dma(reason="one bias value to a partition"):
-            nc.scalar.dma_start(out=bias[:], in_=bg.rearrange("(c p) -> p c", p=P))
+        nc.scalar.dma_start(out=bias_rows[0:4, :], in_=bg.rearrange("(c p) -> c p", p=P))
         nc.sync.dma_start(out=tab_w[:], in_=tab_words[0].rearrange("p t b -> p (t b)").bitcast(I32))
         load_scale_rows(nc.sync, tab_sc, tab_scales)
         nc.scalar.activation(out=zero[:], in_=zero_in[:], func=ACT.Sigmoid)
@@ -95,7 +98,14 @@ def tile_list_hwayt_qf_silu_kernel(
             )
         load_rec(3)
 
-        nc.scalar.activation(out=neg_bias[:], in_=bias[:], func=ACT.Identity, scale=-1.0, bias=zero[:])
+        bias_cols = ps.tile([P, P], F32, name="bias_cols", tag="b6")
+        nc.tensor.transpose(bias_cols[:], bias_rows[:], ident[:])
+        nc.scalar.activation(out=neg_bias[:], in_=bias_cols[:, 0:4], func=ACT.Identity, scale=-1.0, bias=zero[:])
+        warm = ps.tile([P, 4, P], F32, name="warm", tag="b7")
+        for w in range(10):
+            nc.tensor.transpose(warm[:, w % 4, :], bias_rows[:], ident[:])
+        for w in range(14):
+            nc.tensor.transpose(warm[:, (w + 2) % 4, :], raw[0][:, w % 4, 0:P], ident[:])
 
         def cols(h):
             return slice(h * HALF, (h + 1) * HALF)
@@ -189,7 +199,6 @@ def tile_list_hwayt_qf_silu_kernel(
         gather_scales(0, 1)
         gather_scales(1, 1)
         quantize_wh8(0)
-        quantize_wh8(1)
         gate(0, HALF, HALF, NARROW, "b2")
         gate(1, HALF, HALF, NARROW, "b3")
         gate(2, 0, J, J, "b4")
@@ -199,6 +208,7 @@ def tile_list_hwayt_qf_silu_kernel(
         keep(0, 16, 32)
         keep(1, 16, 32)
         keep(2, 0, 32)
+        quantize_wh8(1)
         keep(3, 0, 32)
         hidden(0, "b6")
         hidden(1, "b7")

@@ -64,10 +64,10 @@ def tile_list_hwayt_qf_silu_kernel(
         nc.vector.memset(wh4_sc[:], 0)
 
         def load_scale_rows(queue, plane, rows):
-            for q in range(4):
+            for r in range(4):
                 queue.dma_start(
-                    out=plane[32 * q : 32 * q + 4],
-                    in_=rows[:, 4 * q : 4 * q + 4, :].rearrange("a r t -> r a t").bitcast(I32),
+                    out=plane[r:P:32],
+                    in_=rows[:, r:16:4, :].rearrange("a q t -> q a t").bitcast(I32),
                 )
 
         def load_wh8(u):
@@ -79,9 +79,9 @@ def tile_list_hwayt_qf_silu_kernel(
         def load_rec(c):
             nc.sync.dma_start(out=rec[c][:], in_=rT[c * P : (c + 1) * P, :])
 
-        nc.sync.dma_start(offsets[:], offs)
         nc.scalar.dma_start(out=bias_rows[0:4, :], in_=bg.rearrange("(c p) -> c p", p=P))
         nc.sync.dma_start(out=tab_w[:], in_=tab_words[0].rearrange("p t b -> p (t b)").bitcast(I32))
+        nc.sync.dma_start(offsets[:], offs)
         load_scale_rows(nc.sync, tab_sc, tab_scales)
         nc.scalar.activation(out=zero[:], in_=zero_in[:], func=ACT.Sigmoid)
         load_wh8(0)
@@ -92,10 +92,8 @@ def tile_list_hwayt_qf_silu_kernel(
         load_rec(1)
         load_rec(2)
         nc.sync.dma_start(out=wh4_w[:], in_=wh4_words[0].bitcast(I32))
-        for q in range(4):
-            nc.sync.dma_start(
-                out=wh4_sc[32 * q : 32 * q + 4, :], in_=wh4_scales[0, 4 * q : 4 * q + 4, :].bitcast(I32)
-            )
+        for r in range(4):
+            nc.sync.dma_start(out=wh4_sc[r:P:32, :], in_=wh4_scales[0, r:16:4, :].bitcast(I32))
         load_rec(3)
 
         bias_cols = ps.tile([P, P], F32, name="bias_cols", tag="b6")
@@ -179,17 +177,21 @@ def tile_list_hwayt_qf_silu_kernel(
                 out=kept[c][:, js], in0=rec[c][:].indirect(offsets[:, c0:c1]), in1=carry[c][:, js], op=ALU.mult
             )
 
-        def make(c):
+        def make(c, js):
             nc.vector.scalar_tensor_tensor(
-                out=made[c][:], in0=carry[c][:], scalar=1.0, in1=act[c][:], op0=ALU.subtract, op1=ALU.mult
+                out=made[c][:, js], in0=carry[c][:, js], scalar=1.0, in1=act[c][:, js], op0=ALU.subtract, op1=ALU.mult
             )
 
         def finish(c, js, queue):
             nc.vector.tensor_tensor(out=res[c][:, js], in0=kept[c][:, js], in1=made[c][:, js], op=ALU.subtract)
             queue.dma_start(out=out[c * P : (c + 1) * P, js], in_=res[c][:, js])
 
-        nc.vector.tensor_copy(out=got_w[:], in_=tab_w[:].bitcast(U32).indirect(offsets[:]))
-        nc.vector.tensor_copy(out=item_w[:], in_=got_w[:].bitcast(U16).rearrange("p (j d) -> p d j", d=2))
+        for h in range(2):
+            nc.vector.tensor_copy(out=got_w[:, cols(h)], in_=tab_w[:].bitcast(U32).indirect(offs_of(h)))
+        for h in range(2):
+            nc.vector.tensor_copy(
+                out=item_w[:, :, cols(h)], in_=got_w[:, cols(h)].bitcast(U16).rearrange("p (j d) -> p d j", d=2)
+            )
         gather_scales(0, 0)
         gather_scales(1, 0)
         round_wh8(0)
@@ -214,12 +216,14 @@ def tile_list_hwayt_qf_silu_kernel(
         hidden(1, "b7")
         hidden(2, "b0")
         hidden(3, "b1")
-        make(0)
-        make(1)
-        finish(0, slice(0, J), nc.sync)
-        make(2)
-        finish(1, slice(0, J), nc.sync)
-        make(3)
-        finish(2, slice(0, J), nc.sync)
+        whole = slice(0, J)
+        make(0, whole)
+        make(1, whole)
+        finish(0, whole, nc.sync)
+        make(2, whole)
+        finish(1, whole, nc.sync)
+        make(3, cols(0))
+        finish(2, whole, nc.sync)
+        make(3, cols(1))
         finish(3, cols(0), nc.sync)
         finish(3, cols(1), nc.scalar)

@@ -19,7 +19,6 @@ ALU = mybir.AluOpType
 
 P = 128
 HALF = J // 2
-NARROW = 128
 
 
 def tile_list_hwayt_qf_silu_kernel(
@@ -39,191 +38,192 @@ def tile_list_hwayt_qf_silu_kernel(
         wh4_w = sb.tile([P, N // 2], I32, name="wh4_w", align_bytes=64)
         bias_rows = sb.tile([P, P], F32, name="bias_rows")
         ident = sb.tile([P, P], F32, name="ident")
-        neg_bias = sb.tile([P, 4], F32, name="neg_bias")
+        half_bias = sb.tile([P, 4], F32, name="half_bias")
         zero_in = sb.tile([P, 1], F32, name="zero_in")
         zero = sb.tile([P, 1], F32, name="zero")
-        raw = [sb.tile([P, 4, N // 2], F32, name="raw%d" % u, align_bytes=64) for u in range(2)]
-        grouped = [sb.tile([P, N // 2, 4], BF16, name="grouped%d" % u, align_bytes=64) for u in range(2)]
-        wh8_w = [sb.tile([P, N // 2], U32, name="wh8_w%d" % u, align_bytes=64) for u in range(2)]
-        wh8_sc = [sb.tile([P, N // 2], U8, name="wh8_sc%d" % u, align_bytes=64) for u in range(2)]
+        raw = [sb.tile([P, 4, w], F32, name="raw%d" % w, align_bytes=64) for w in (P, N - P)]
+        grouped = [sb.tile([P, P, 4], BF16, name="grouped%d" % c, align_bytes=64) for c in range(4)]
+        wh8_w = [sb.tile([P, P], U32, name="wh8_w%d" % c, align_bytes=64) for c in range(4)]
+        wh8_sc = [sb.tile([P, P], U8, name="wh8_sc%d" % c, align_bytes=64) for c in range(4)]
         rec = [sb.tile([P, T], F32, name="rec%d" % c, align_bytes=64) for c in range(4)]
         got_w = sb.tile([P, J], U32, name="got_w", align_bytes=64)
         got_sc = sb.tile([P, 2, J], U8, name="got_sc", align_bytes=64)
         item_w = sb.tile([P, 2, J], U16, name="item_w", align_bytes=64)
-        carry = [sb.tile([P, J], F32, name="carry%d" % c) for c in range(4)]
+        lean = [sb.tile([P, J], F32, name="lean%d" % c) for c in range(4)]
         act = [sb.tile([P, J], F32, name="act%d" % c) for c in range(4)]
-        kept = [sb.tile([P, J], F32, name="kept%d" % c) for c in range(4)]
-        made = [sb.tile([P, J], F32, name="made%d" % c) for c in range(4)]
+        diff = {}
+        part = [sb.tile([P, J], F32, name="part%d" % c) for c in range(4)]
         res = [sb.tile([P, J], F32, name="res%d" % c) for c in range(4)]
+        item_sc = [got_sc[:, 0, :], got_sc[:, 1, :]]
 
         nc.vector.memset(tab_sc[:], 0)
-        nc.gpsimd.memset(bias_rows[:], 0.0)
-        nc.gpsimd.memset(zero_in[:], -200.0)
-        make_identity(nc, ident[:])
-        nc.vector.memset(wg_sc[:], 0)
         nc.vector.memset(wh4_sc[:], 0)
-
-        def load_scale_rows(queue, plane, rows):
-            for r in range(4):
-                queue.dma_start(
-                    out=plane[r:P:32],
-                    in_=rows[:, r:16:4, :].rearrange("a q t -> q a t").bitcast(I32),
-                )
+        nc.vector.memset(wg_sc[:], 0)
+        nc.gpsimd.memset(bias_rows[:], 0.0)
+        nc.gpsimd.memset(zero_in[:], 0.0)
+        make_identity(nc, ident[:])
 
         def load_wh8(u):
             nc.sync.dma_start(
                 out=raw[u][:],
-                in_=wh8[:, u * 256 : (u + 1) * 256].rearrange("(p i) n -> p i n", i=4),
+                in_=wh8[:, u * P : P + u * (N - P)].rearrange("(p i) n -> p i n", i=4),
             )
 
         def load_rec(c):
             nc.sync.dma_start(out=rec[c][:], in_=rT[c * P : (c + 1) * P, :])
 
-        nc.scalar.dma_start(out=bias_rows[0:4, :], in_=bg.rearrange("(c p) -> c p", p=P))
         nc.sync.dma_start(out=tab_w[:], in_=tab_words[0].rearrange("p t b -> p (t b)").bitcast(I32))
         nc.sync.dma_start(offsets[:], offs)
-        load_scale_rows(nc.sync, tab_sc, tab_scales)
-        nc.scalar.activation(out=zero[:], in_=zero_in[:], func=ACT.Sigmoid)
         load_wh8(0)
+        for r in range(4):
+            nc.sync.dma_start(
+                out=tab_sc[r:P:32], in_=tab_scales[:, r:16:4, :].rearrange("a q t -> q a t").bitcast(I32)
+            )
+        nc.scalar.activation(out=zero[:], in_=zero_in[:], func=ACT.Silu)
         load_wh8(1)
-        load_scale_rows(nc.sync, wg_sc, wg_scales)
-        nc.sync.dma_start(out=wg_w[:], in_=wg_words.rearrange("a p n i -> p a (n i)").bitcast(I32))
-        load_rec(0)
-        load_rec(1)
-        load_rec(2)
         nc.sync.dma_start(out=wh4_w[:], in_=wh4_words[0].bitcast(I32))
         for r in range(4):
             nc.sync.dma_start(out=wh4_sc[r:P:32, :], in_=wh4_scales[0, r:16:4, :].bitcast(I32))
+        load_rec(0)
+        load_rec(1)
+        for r in range(4):
+            nc.sync.dma_start(
+                out=wg_sc[r:P:32], in_=wg_scales[:, r:16:4, :].rearrange("a q t -> q a t").bitcast(I32)
+            )
+        nc.sync.dma_start(out=wg_w[:], in_=wg_words.rearrange("a p n i -> p a (n i)").bitcast(I32))
+        nc.sync.dma_start(out=bias_rows[0:4, :], in_=bg.rearrange("(c p) -> c p", p=P))
+        load_rec(2)
         load_rec(3)
 
-        bias_cols = ps.tile([P, P], F32, name="bias_cols", tag="b6")
+        bias_cols = ps.tile([P, P], F32, name="bias_cols", tag="b7")
         nc.tensor.transpose(bias_cols[:], bias_rows[:], ident[:])
-        nc.scalar.activation(out=neg_bias[:], in_=bias_cols[:, 0:4], func=ACT.Identity, scale=-1.0, bias=zero[:])
-        warm = ps.tile([P, 4, P], F32, name="warm", tag="b7")
-        for w in range(10):
-            nc.tensor.transpose(warm[:, w % 4, :], bias_rows[:], ident[:])
-        for w in range(14):
-            nc.tensor.transpose(warm[:, (w + 2) % 4, :], raw[0][:, w % 4, 0:P], ident[:])
+        nc.scalar.activation(out=half_bias[:], in_=bias_cols[:, 0:4], func=ACT.Identity, scale=-0.5, bias=zero[:])
 
         def cols(h):
             return slice(h * HALF, (h + 1) * HALF)
 
-        def offs_of(h):
-            return offsets[:, h * (HALF // 16) : (h + 1) * (HALF // 16)]
+        whole = slice(0, J)
 
-        def gather_scales(a, h):
-            nc.vector.tensor_copy(
-                out=got_sc[:, a, cols(h)], in_=tab_sc[:, a, :].bitcast(U8).indirect(offs_of(h))
-            )
+        def offs_of(js):
+            return offsets[:, js.start // 16 : js.stop // 16]
 
-        def round_wh8(u):
+        def gather_scales(a, js):
+            nc.vector.tensor_copy(out=got_sc[:, a, js], in_=tab_sc[:, a, :].bitcast(U8).indirect(offs_of(js)))
+
+        def round_wh8(c):
+            u, m = min(c, 1), max(c - 1, 0)
             nc.scalar.copy(
-                out=grouped[u][:].rearrange("p (c m) i -> p c i m", m=4),
-                in_=raw[u][:].rearrange("p i (c m) -> p c i m", m=4),
+                out=grouped[c][:].rearrange("p (g m) i -> p g i m", m=4),
+                in_=raw[u][:, :, m * P : (m + 1) * P].rearrange("p i (g m) -> p g i m", m=4),
             )
 
-        def quantize_wh8(u):
+        def quantize_wh8(c):
             nc.vector.quantize_mx(
-                out=wh8_w[u][:].bitcast(FP8X4),
-                scales=wh8_sc[u][:],
-                in_=grouped[u][:].rearrange("p n i -> p (n i)"),
+                out=wh8_w[c][:].bitcast(FP8X4),
+                scales=wh8_sc[c][:],
+                in_=grouped[c][:].rearrange("p n i -> p (n i)"),
             )
 
-        def gate(c, j0, width, step, tag):
-            acc = ps.tile([P, width], F32, name="ga", tag=tag)
-            for s in range(0, width, step):
-                js = slice(j0 + s, j0 + s + step)
-                for a in range(2):
-                    nc.tensor.matmul_mx(
-                        out=acc[:, s : s + step],
-                        lhsT=wg_w[:, a, c * P : (c + 1) * P].bitcast(FP8X4),
-                        lhsT_scale=wg_sc[:, a, c * 32 : (c + 1) * 32].bitcast(U8),
-                        rhs=item_w[:, a, js].bitcast(FP4X4),
-                        rhs_scale=got_sc[:, a, js],
-                        start=(a == 0),
-                        stop=(a == 1),
-                    )
-            js = slice(j0, j0 + width)
-            nc.scalar.activation(
-                out=carry[c][:, js], in_=acc[:], func=ACT.Sigmoid, bias=neg_bias[:, c : c + 1], scale=-1.0
-            )
+        def gate(c, tag):
+            acc = ps.tile([P, J], F32, name="ga", tag=tag)
+            for a in range(2):
+                nc.tensor.matmul_mx(
+                    out=acc[:],
+                    lhsT=wg_w[:, a, c * P : (c + 1) * P].bitcast(FP8X4),
+                    lhsT_scale=wg_sc[:, a, c * 32 : (c + 1) * 32].bitcast(U8),
+                    rhs=item_w[:, a, :].bitcast(FP4X4),
+                    rhs_scale=item_sc[a],
+                    start=(a == 0),
+                    stop=(a == 1),
+                )
+            nc.scalar.activation(out=lean[c][:], in_=acc[:], func=ACT.Tanh, bias=half_bias[:, c : c + 1], scale=-0.5)
 
-        def hidden(c, tag):
-            acc = ps.tile([P, J], F32, name="ha", tag=tag)
-            u, m = divmod(c, 2)
+        def hidden_open(c, js, tag):
+            acc = ps.tile([P, js.stop - js.start], F32, name="ha", tag=tag)
             nc.tensor.matmul_mx(
                 out=acc[:],
                 lhsT=wh4_w[:, c * 64 : (c + 1) * 64].bitcast(FP4X4),
                 lhsT_scale=wh4_sc[:, c * 32 : (c + 1) * 32].bitcast(U8),
-                rhs=item_w[:, 1, :].bitcast(FP4X4),
-                rhs_scale=got_sc[:, 1, :],
+                rhs=item_w[:, 1, js].bitcast(FP4X4),
+                rhs_scale=item_sc[1][:, js],
                 start=True,
                 stop=False,
             )
-            nc.tensor.matmul_mx(
-                out=acc[:],
-                lhsT=wh8_w[u][:, m * P : (m + 1) * P].bitcast(FP8X4),
-                lhsT_scale=wh8_sc[u][:, m * P : (m + 1) * P],
-                rhs=item_w[:, 0, :].bitcast(FP4X4),
-                rhs_scale=got_sc[:, 0, :],
-                start=False,
-                stop=True,
-            )
-            nc.scalar.activation(out=act[c][:], in_=acc[:], func=ACT.Silu)
+            return acc
 
-        def keep(c, c0, c1):
-            js = slice(16 * c0, 16 * c1)
+        def hidden_close(c, js, step, acc):
+            width = js.stop - js.start
+            for s in range(0, width, step):
+                nc.tensor.matmul_mx(
+                    out=acc[:, s : s + step],
+                    lhsT=wh8_w[c][:].bitcast(FP8X4),
+                    lhsT_scale=wh8_sc[c][:],
+                    rhs=item_w[:, 0, js.start + s : js.start + s + step].bitcast(FP4X4),
+                    rhs_scale=item_sc[0][:, js.start + s : js.start + s + step],
+                    start=False,
+                    stop=(s + step == width),
+                )
+            nc.scalar.activation(out=act[c][:, js], in_=acc[:], func=ACT.Silu)
+
+        def differ(c, js):
+            if c not in diff:
+                diff[c] = sb.tile([P, J], F32, name="diff", tag="diff%d" % (1 if c == 3 else c))
             nc.vector.tensor_tensor(
-                out=kept[c][:, js], in0=rec[c][:].indirect(offsets[:, c0:c1]), in1=carry[c][:, js], op=ALU.mult
+                out=diff[c][:, js], in0=rec[c][:].indirect(offs_of(js)), in1=act[c][:, js], op=ALU.subtract
             )
 
-        def make(c, js):
+        def weigh(c, js):
             nc.vector.scalar_tensor_tensor(
-                out=made[c][:, js], in0=carry[c][:, js], scalar=1.0, in1=act[c][:, js], op0=ALU.subtract, op1=ALU.mult
+                out=part[c][:, js], in0=lean[c][:, js], scalar=1.0, in1=diff[c][:, js], op0=ALU.add, op1=ALU.mult
             )
 
         def finish(c, js, queue):
-            nc.vector.tensor_tensor(out=res[c][:, js], in0=kept[c][:, js], in1=made[c][:, js], op=ALU.subtract)
+            nc.vector.scalar_tensor_tensor(
+                out=res[c][:, js], in0=part[c][:, js], scalar=0.5, in1=act[c][:, js], op0=ALU.mult, op1=ALU.add
+            )
             queue.dma_start(out=out[c * P : (c + 1) * P, js], in_=res[c][:, js])
 
+        round_wh8(0)
+        round_wh8(1)
         for h in range(2):
-            nc.vector.tensor_copy(out=got_w[:, cols(h)], in_=tab_w[:].bitcast(U32).indirect(offs_of(h)))
+            nc.vector.tensor_copy(out=got_w[:, cols(h)], in_=tab_w[:].bitcast(U32).indirect(offs_of(cols(h))))
         for h in range(2):
             nc.vector.tensor_copy(
                 out=item_w[:, :, cols(h)], in_=got_w[:, cols(h)].bitcast(U16).rearrange("p (j d) -> p d j", d=2)
             )
-        gather_scales(0, 0)
-        gather_scales(1, 0)
-        round_wh8(0)
-        round_wh8(1)
-        gate(0, 0, HALF, NARROW, "b0")
-        gate(1, 0, HALF, NARROW, "b1")
-        gather_scales(0, 1)
-        gather_scales(1, 1)
         quantize_wh8(0)
-        gate(0, HALF, HALF, NARROW, "b2")
-        gate(1, HALF, HALF, NARROW, "b3")
-        gate(2, 0, J, J, "b4")
-        gate(3, 0, J, J, "b5")
-        keep(0, 0, 16)
-        keep(1, 0, 16)
-        keep(0, 16, 32)
-        keep(1, 16, 32)
-        keep(2, 0, 32)
+        for h in range(2):
+            gather_scales(1, cols(h))
+            gather_scales(0, cols(h))
+        round_wh8(2)
+        round_wh8(3)
         quantize_wh8(1)
-        keep(3, 0, 32)
-        hidden(0, "b6")
-        hidden(1, "b7")
-        hidden(2, "b0")
-        hidden(3, "b1")
-        whole = slice(0, J)
-        make(0, whole)
-        make(1, whole)
+        quantize_wh8(2)
+        quantize_wh8(3)
+        first = [hidden_open(c, cols(0), "b%d" % c) for c in range(2)]
+        hidden_close(0, cols(0), P, first[0])
+        second = [hidden_open(c, cols(1), "b%d" % (2 + c)) for c in range(2)]
+        hidden_close(0, cols(1), P, second[0])
+        hidden_close(1, cols(0), P, first[1])
+        hidden_close(1, cols(1), P, second[1])
+        for c in range(2):
+            for h in range(2):
+                differ(c, cols(h))
+        hidden_close(2, whole, J, hidden_open(2, whole, "b4"))
+        gate(0, "b5")
+        gate(1, "b6")
+        gate(2, "b7")
+        hidden_close(3, whole, J, hidden_open(3, whole, "b5"))
+        gate(3, "b0")
+        weigh(0, whole)
+        differ(2, whole)
+        weigh(1, whole)
         finish(0, whole, nc.sync)
-        make(2, whole)
+        weigh(2, whole)
+        differ(3, whole)
         finish(1, whole, nc.sync)
-        make(3, cols(0))
+        weigh(3, cols(0))
         finish(2, whole, nc.sync)
-        make(3, cols(1))
+        weigh(3, cols(1))
         finish(3, cols(0), nc.sync)
         finish(3, cols(1), nc.scalar)

@@ -54,6 +54,7 @@ def tile_list_hwayt_qf_silu_kernel(
         diff = {}
         part = [sb.tile([P, J], F32, name="part%d" % c) for c in range(4)]
         res = [sb.tile([P, J], F32, name="res%d" % c) for c in range(4)]
+        turned = [sb.tile([P, 4, P], F32, name="turned%d" % c) for c in range(2)]
         item_sc = [got_sc[:, 0, :], got_sc[:, 1, :]]
 
         nc.vector.memset(tab_sc[:], 0)
@@ -183,6 +184,34 @@ def tile_list_hwayt_qf_silu_kernel(
             )
             queue.dma_start(out=out[c * P : (c + 1) * P, js], in_=res[c][:, js])
 
+        def add_turned(acc, term, start, stop):
+            for b in range(4):
+                nc.tensor.matmul(
+                    acc[:, b, :],
+                    term[:, b * P : (b + 1) * P],
+                    ident[:],
+                    is_transpose=True,
+                    start=(start and b == 0),
+                    stop=(stop and b == 3),
+                )
+
+        def sum_open(c, tag):
+            acc = ps.tile([P, 4, P], F32, name="sum", tag=tag)
+            add_turned(acc, act[c], True, False)
+            add_turned(acc, act[c], False, False)
+            return acc
+
+        def sum_close(c, acc):
+            add_turned(acc, part[c], False, True)
+            nc.scalar.activation(out=turned[c][:], in_=acc[:], func=ACT.Copy, scale=0.5)
+
+        def turn_back(c, tag):
+            acc = ps.tile([P, 4, P], F32, name="back", tag=tag)
+            for b in range(4):
+                nc.tensor.transpose(acc[:, b, :], turned[c][:, b, :], ident[:])
+            nc.scalar.copy(out=res[c][:], in_=acc[:].rearrange("p b j -> p (b j)"))
+            nc.sync.dma_start(out=out[c * P : (c + 1) * P, :], in_=res[c][:])
+
         round_wh8(0)
         round_wh8(1)
         for h in range(2):
@@ -214,14 +243,17 @@ def tile_list_hwayt_qf_silu_kernel(
         gate(1, "b6")
         gate(2, "b7")
         hidden_close(3, whole, J, hidden_open(3, whole, "b5"))
+        sum0 = sum_open(0, "b6")
         gate(3, "b0")
-        weigh(0, whole)
         differ(2, whole)
+        weigh(0, whole)
         weigh(1, whole)
-        finish(0, whole, nc.sync)
         weigh(2, whole)
         differ(3, whole)
-        finish(1, whole, nc.sync)
+        sum_close(0, sum0)
+        sum_close(1, sum_open(1, "b7"))
+        turn_back(0, "b1")
+        turn_back(1, "b2")
         weigh(3, cols(0))
         finish(2, whole, nc.sync)
         weigh(3, cols(1))

@@ -54,7 +54,7 @@ def tile_list_hwayt_qf_silu_kernel(
         diff = {}
         part = [sb.tile([P, J], F32, name="part%d" % c) for c in range(4)]
         res = [sb.tile([P, J], F32, name="res%d" % c) for c in range(4)]
-        turned = [sb.tile([P, 4, P], F32, name="turned%d" % c) for c in range(2)]
+        turned = [sb.tile([P, 4, P], F32, name="turned%d" % c) for c in range(1)]
         item_sc = [got_sc[:, 0, :], got_sc[:, 1, :]]
 
         nc.vector.memset(tab_sc[:], 0)
@@ -168,7 +168,7 @@ def tile_list_hwayt_qf_silu_kernel(
 
         def differ(c, js):
             if c not in diff:
-                diff[c] = sb.tile([P, J], F32, name="diff", tag="diff%d" % (1 if c == 3 else c))
+                diff[c] = sb.tile([P, J], F32, name="diff", tag="diff%d" % min(c, 2))
             nc.vector.tensor_tensor(
                 out=diff[c][:, js], in0=rec[c][:].indirect(offs_of(js)), in1=act[c][:, js], op=ALU.subtract
             )
@@ -210,7 +210,7 @@ def tile_list_hwayt_qf_silu_kernel(
             for b in range(4):
                 nc.tensor.transpose(acc[:, b, :], turned[c][:, b, :], ident[:])
             nc.scalar.copy(out=res[c][:], in_=acc[:].rearrange("p b j -> p (b j)"))
-            nc.sync.dma_start(out=out[c * P : (c + 1) * P, :], in_=res[c][:])
+            nc.scalar.dma_start(out=out[c * P : (c + 1) * P, :], in_=res[c][:])
 
         round_wh8(0)
         round_wh8(1)
@@ -249,13 +249,12 @@ def tile_list_hwayt_qf_silu_kernel(
         weigh(0, whole)
         weigh(1, whole)
         weigh(2, whole)
-        differ(3, whole)
         sum_close(0, sum0)
-        sum_close(1, sum_open(1, "b7"))
         turn_back(0, "b1")
-        turn_back(1, "b2")
-        weigh(3, cols(0))
+        finish(1, whole, nc.sync)
         finish(2, whole, nc.sync)
-        weigh(3, cols(1))
-        finish(3, cols(0), nc.sync)
-        finish(3, cols(1), nc.scalar)
+        for step in (differ, weigh):
+            for h in range(2):
+                step(3, cols(h))
+        for h in range(2):
+            finish(3, cols(h), nc.sync)

@@ -33,7 +33,7 @@ def tile_list_hwayt_qf_silu_kernel(
         tab_sc = sb.tile([P, 2, T // 4], I32, name="tab_sc", align_bytes=64)
         tab_w = sb.tile([P, T], I32, name="tab_w", align_bytes=64)
         wg_sc = sb.tile([P, 2, N // 4], I32, name="wg_sc", align_bytes=64)
-        wg_w = sb.tile([P, 2, N], I32, name="wg_w", align_bytes=64)
+        wg_w = [sb.tile([P, 2, N // 2], I32, name="wg_w%d" % u, align_bytes=64) for u in range(2)]
         wh4_sc = sb.tile([P, N // 4], I32, name="wh4_sc", align_bytes=64)
         wh4_w = sb.tile([P, N // 2], I32, name="wh4_w", align_bytes=64)
         bias_rows = sb.tile([P, P], F32, name="bias_rows")
@@ -54,7 +54,7 @@ def tile_list_hwayt_qf_silu_kernel(
         diff = {}
         part = [sb.tile([P, J], F32, name="part%d" % c) for c in range(4)]
         res = [sb.tile([P, J], F32, name="res%d" % c) for c in range(4)]
-        turned = [sb.tile([P, 4, P], F32, name="turned%d" % c) for c in range(1)]
+        turned = sb.tile([P, 4, P], F32, name="turned")
         item_sc = [got_sc[:, 0, :], got_sc[:, 1, :]]
 
         nc.vector.memset(tab_sc[:], 0)
@@ -68,6 +68,12 @@ def tile_list_hwayt_qf_silu_kernel(
             nc.sync.dma_start(
                 out=raw[u][:],
                 in_=wh8[:, u * P : P + u * (N - P)].rearrange("(p i) n -> p i n", i=4),
+            )
+
+        def load_wg(u):
+            nc.sync.dma_start(
+                out=wg_w[u][:],
+                in_=wg_words[:, :, u * 256 : (u + 1) * 256, :].rearrange("a p n i -> p a (n i)").bitcast(I32),
             )
 
         def load_rec(c):
@@ -86,13 +92,14 @@ def tile_list_hwayt_qf_silu_kernel(
         for r in range(4):
             nc.sync.dma_start(out=wh4_sc[r:P:32, :], in_=wh4_scales[0, r:16:4, :].bitcast(I32))
         load_rec(0)
+        load_wg(0)
         load_rec(1)
+        nc.sync.dma_start(out=bias_rows[0:4, :], in_=bg.rearrange("(c p) -> c p", p=P))
         for r in range(4):
             nc.sync.dma_start(
                 out=wg_sc[r:P:32], in_=wg_scales[:, r:16:4, :].rearrange("a q t -> q a t").bitcast(I32)
             )
-        nc.sync.dma_start(out=wg_w[:], in_=wg_words.rearrange("a p n i -> p a (n i)").bitcast(I32))
-        nc.sync.dma_start(out=bias_rows[0:4, :], in_=bg.rearrange("(c p) -> c p", p=P))
+        load_wg(1)
         load_rec(2)
         load_rec(3)
 
@@ -130,7 +137,7 @@ def tile_list_hwayt_qf_silu_kernel(
             for a in range(2):
                 nc.tensor.matmul_mx(
                     out=acc[:],
-                    lhsT=wg_w[:, a, c * P : (c + 1) * P].bitcast(FP8X4),
+                    lhsT=wg_w[c // 2][:, a, (c % 2) * P : (c % 2 + 1) * P].bitcast(FP8X4),
                     lhsT_scale=wg_sc[:, a, c * 32 : (c + 1) * 32].bitcast(U8),
                     rhs=item_w[:, a, :].bitcast(FP4X4),
                     rhs_scale=item_sc[a],
@@ -168,7 +175,7 @@ def tile_list_hwayt_qf_silu_kernel(
 
         def differ(c, js):
             if c not in diff:
-                diff[c] = sb.tile([P, J], F32, name="diff", tag="diff%d" % min(c, 2))
+                diff[c] = sb.tile([P, J], F32, name="diff", tag="diff%d" % (c % 2))
             nc.vector.tensor_tensor(
                 out=diff[c][:, js], in0=rec[c][:].indirect(offs_of(js)), in1=act[c][:, js], op=ALU.subtract
             )
@@ -203,12 +210,12 @@ def tile_list_hwayt_qf_silu_kernel(
 
         def sum_close(c, acc):
             add_turned(acc, part[c], False, True)
-            nc.scalar.activation(out=turned[c][:], in_=acc[:], func=ACT.Copy, scale=0.5)
+            nc.scalar.activation(out=turned[:], in_=acc[:], func=ACT.Copy, scale=0.5)
 
         def turn_back(c, tag):
             acc = ps.tile([P, 4, P], F32, name="back", tag=tag)
             for b in range(4):
-                nc.tensor.transpose(acc[:, b, :], turned[c][:, b, :], ident[:])
+                nc.tensor.transpose(acc[:, b, :], turned[:, b, :], ident[:])
             nc.scalar.copy(out=res[c][:], in_=acc[:].rearrange("p b j -> p (b j)"))
             nc.scalar.dma_start(out=out[c * P : (c + 1) * P, :], in_=res[c][:])
 
@@ -238,23 +245,22 @@ def tile_list_hwayt_qf_silu_kernel(
         for c in range(2):
             for h in range(2):
                 differ(c, cols(h))
-        hidden_close(2, whole, J, hidden_open(2, whole, "b4"))
-        gate(0, "b5")
-        gate(1, "b6")
-        gate(2, "b7")
-        hidden_close(3, whole, J, hidden_open(3, whole, "b5"))
-        sum0 = sum_open(0, "b6")
-        gate(3, "b0")
-        differ(2, whole)
+        hidden_close(2, whole, J, hidden_open(2, whole, "b6"))
+        gate(0, "b4")
+        gate(1, "b5")
+        hidden_close(3, whole, J, hidden_open(3, whole, "b4"))
+        gate(2, "b0")
+        gate(3, "b1")
         weigh(0, whole)
         weigh(1, whole)
+        finish(0, whole, nc.sync)
+        sum_close(1, sum_open(1, "b5"))
+        turn_back(1, "b2")
+        differ(2, whole)
+        differ(3, whole)
         weigh(2, whole)
-        sum_close(0, sum0)
-        turn_back(0, "b1")
-        finish(1, whole, nc.sync)
+        weigh(3, cols(0))
         finish(2, whole, nc.sync)
-        for step in (differ, weigh):
-            for h in range(2):
-                step(3, cols(h))
+        weigh(3, cols(1))
         for h in range(2):
             finish(3, cols(h), nc.sync)

@@ -52,9 +52,9 @@ def tile_list_hwayt_qf_silu_kernel(
         lean = [sb.tile([P, J], F32, name="lean%d" % c) for c in range(4)]
         act = [sb.tile([P, J], F32, name="act%d" % c) for c in range(4)]
         diff = {}
-        part = [sb.tile([P, J], F32, name="part%d" % c) for c in range(4)]
-        res = [sb.tile([P, J], F32, name="res%d" % c) for c in range(4)]
-        turned = sb.tile([P, 4, P], F32, name="turned")
+        part = {}
+        res = [sb.tile([P, J], F32, name="res%d" % c) for c in range(3)]
+        turned = [sb.tile([P, 2, P], F32, name="turned", tag="turned%d" % h) for h in range(2)]
         item_sc = [got_sc[:, 0, :], got_sc[:, 1, :]]
 
         nc.vector.memset(tab_sc[:], 0)
@@ -180,14 +180,15 @@ def tile_list_hwayt_qf_silu_kernel(
                 out=diff[c][:, js], in0=rec[c][:].indirect(offs_of(js)), in1=act[c][:, js], op=ALU.subtract
             )
 
-        def weigh(c, js):
+        def weigh(c, js, tag):
+            part[c, js.start] = sb.tile([P, js.stop - js.start], F32, name="part", tag=tag)
             nc.vector.scalar_tensor_tensor(
-                out=part[c][:, js], in0=lean[c][:, js], scalar=1.0, in1=diff[c][:, js], op0=ALU.add, op1=ALU.mult
+                out=part[c, js.start][:], in0=lean[c][:, js], scalar=1.0, in1=diff[c][:, js], op0=ALU.add, op1=ALU.mult
             )
 
         def finish(c, js, queue):
             nc.vector.scalar_tensor_tensor(
-                out=res[c][:, js], in0=part[c][:, js], scalar=0.5, in1=act[c][:, js], op0=ALU.mult, op1=ALU.add
+                out=res[c][:, js], in0=part[c, js.start][:], scalar=0.5, in1=act[c][:, js], op0=ALU.mult, op1=ALU.add
             )
             queue.dma_start(out=out[c * P : (c + 1) * P, js], in_=res[c][:, js])
 
@@ -209,13 +210,14 @@ def tile_list_hwayt_qf_silu_kernel(
             return acc
 
         def sum_close(c, acc):
-            add_turned(acc, part[c], False, True)
-            nc.scalar.activation(out=turned[:], in_=acc[:], func=ACT.Copy, scale=0.5)
+            add_turned(acc, part[c, 0], False, True)
+            for h in range(2):
+                nc.scalar.activation(out=turned[h][:], in_=acc[:, 2 * h : 2 * h + 2, :], func=ACT.Copy, scale=0.5)
 
         def turn_back(c, tag):
             acc = ps.tile([P, 4, P], F32, name="back", tag=tag)
             for b in range(4):
-                nc.tensor.transpose(acc[:, b, :], turned[:, b, :], ident[:])
+                nc.tensor.transpose(acc[:, b, :], turned[b // 2][:, b % 2, :], ident[:])
             nc.scalar.copy(out=res[c][:], in_=acc[:].rearrange("p b j -> p (b j)"))
             nc.scalar.dma_start(out=out[c * P : (c + 1) * P, :], in_=res[c][:])
 
@@ -251,16 +253,17 @@ def tile_list_hwayt_qf_silu_kernel(
         hidden_close(3, whole, J, hidden_open(3, whole, "b4"))
         gate(2, "b0")
         gate(3, "b1")
-        weigh(0, whole)
-        weigh(1, whole)
+        weigh(0, whole, "part0")
+        weigh(1, whole, "part1")
         finish(0, whole, nc.sync)
         sum_close(1, sum_open(1, "b5"))
         turn_back(1, "b2")
         differ(2, whole)
         differ(3, whole)
-        weigh(2, whole)
-        weigh(3, cols(0))
+        weigh(2, whole, "part2")
+        weigh(3, cols(0), "part3")
         finish(2, whole, nc.sync)
-        weigh(3, cols(1))
-        for h in range(2):
-            finish(3, cols(h), nc.sync)
+        weigh(3, cols(1), "turned0")
+        res.append(sb.tile([P, J], F32, name="res3", tag="turned1"))
+        finish(3, cols(0), nc.sync)
+        finish(3, cols(1), nc.scalar)

@@ -93,12 +93,12 @@ def tile_list_hwayt_qf_silu_kernel(
             nc.sync.dma_start(out=wh4_sc[r:P:32, :], in_=wh4_scales[0, r:16:4, :].bitcast(I32))
         load_rec(0)
         load_wg(0)
-        load_rec(1)
         nc.sync.dma_start(out=bias_rows[0:4, :], in_=bg.rearrange("(c p) -> c p", p=P))
         for r in range(4):
             nc.sync.dma_start(
                 out=wg_sc[r:P:32], in_=wg_scales[:, r:16:4, :].rearrange("a q t -> q a t").bitcast(I32)
             )
+        load_rec(1)
         load_wg(1)
         load_rec(2)
         load_rec(3)
@@ -146,20 +146,18 @@ def tile_list_hwayt_qf_silu_kernel(
                 )
             nc.scalar.activation(out=lean[c][:], in_=acc[:], func=ACT.Tanh, bias=half_bias[:, c : c + 1], scale=-0.5)
 
-        def hidden_open(c, js, tag):
-            acc = ps.tile([P, js.stop - js.start], F32, name="ha", tag=tag)
+        def wh4_pass(c, js, acc, start, stop):
             nc.tensor.matmul_mx(
                 out=acc[:],
                 lhsT=wh4_w[:, c * 64 : (c + 1) * 64].bitcast(FP4X4),
                 lhsT_scale=wh4_sc[:, c * 32 : (c + 1) * 32].bitcast(U8),
                 rhs=item_w[:, 1, js].bitcast(FP4X4),
                 rhs_scale=item_sc[1][:, js],
-                start=True,
-                stop=False,
+                start=start,
+                stop=stop,
             )
-            return acc
 
-        def hidden_close(c, js, step, acc):
+        def wh8_pass(c, js, step, acc, start, stop):
             width = js.stop - js.start
             for s in range(0, width, step):
                 nc.tensor.matmul_mx(
@@ -168,10 +166,21 @@ def tile_list_hwayt_qf_silu_kernel(
                     lhsT_scale=wh8_sc[c][:],
                     rhs=item_w[:, 0, js.start + s : js.start + s + step].bitcast(FP4X4),
                     rhs_scale=item_sc[0][:, js.start + s : js.start + s + step],
-                    start=False,
-                    stop=(s + step == width),
+                    start=(start and s == 0),
+                    stop=(stop and s + step == width),
                 )
+
+        def silu(c, js, acc):
             nc.scalar.activation(out=act[c][:, js], in_=acc[:], func=ACT.Silu)
+
+        def hidden_open(c, js, tag):
+            acc = ps.tile([P, js.stop - js.start], F32, name="ha", tag=tag)
+            wh4_pass(c, js, acc, True, False)
+            return acc
+
+        def hidden_close(c, js, step, acc):
+            wh8_pass(c, js, step, acc, False, True)
+            silu(c, js, acc)
 
         def differ(c, js):
             if c not in diff:
@@ -231,38 +240,41 @@ def tile_list_hwayt_qf_silu_kernel(
             )
         quantize_wh8(0)
         for h in range(2):
-            gather_scales(1, cols(h))
-            gather_scales(0, cols(h))
+            gather_scales(h, cols(h))
+            gather_scales(1 - h, cols(h))
         round_wh8(2)
         round_wh8(3)
         quantize_wh8(1)
         quantize_wh8(2)
         quantize_wh8(3)
-        first = [hidden_open(c, cols(0), "b%d" % c) for c in range(2)]
-        hidden_close(0, cols(0), P, first[0])
-        second = [hidden_open(c, cols(1), "b%d" % (2 + c)) for c in range(2)]
-        hidden_close(0, cols(1), P, second[0])
-        hidden_close(1, cols(0), P, first[1])
-        hidden_close(1, cols(1), P, second[1])
+        first = ps.tile([P, HALF], F32, name="ha", tag="b0")
+        wh8_pass(0, cols(0), P, first, True, False)
+        wh4_pass(0, cols(0), first, False, True)
+        silu(0, cols(0), first)
+        opened = [hidden_open(c, cols(h), "b%d" % (c + 2 * h)) for c, h in ((1, 0), (0, 1), (1, 1))]
+        hidden_close(0, cols(1), P, opened[1])
+        hidden_close(1, cols(0), P, opened[0])
+        hidden_close(1, cols(1), P, opened[2])
         for c in range(2):
             for h in range(2):
                 differ(c, cols(h))
-        hidden_close(2, whole, J, hidden_open(2, whole, "b6"))
         gate(0, "b4")
         gate(1, "b5")
-        hidden_close(3, whole, J, hidden_open(3, whole, "b4"))
+        hidden_close(2, whole, J, hidden_open(2, whole, "b4"))
+        hidden_close(3, whole, J, hidden_open(3, whole, "b5"))
         gate(2, "b0")
-        gate(3, "b1")
         weigh(0, whole, "part0")
         weigh(1, whole, "part1")
-        finish(0, whole, nc.sync)
-        sum_close(1, sum_open(1, "b5"))
+        sum_close(1, sum_open(1, "b4"))
+        gate(3, "b5")
         turn_back(1, "b2")
         differ(2, whole)
-        differ(3, whole)
+        finish(0, whole, nc.sync)
         weigh(2, whole, "part2")
-        weigh(3, cols(0), "part3")
+        differ(3, cols(0))
         finish(2, whole, nc.sync)
+        differ(3, cols(1))
+        weigh(3, cols(0), "part3")
         weigh(3, cols(1), "turned0")
         res.append(sb.tile([P, J], F32, name="res3", tag="turned1"))
         finish(3, cols(0), nc.sync)

@@ -93,12 +93,12 @@ def tile_list_hwayt_qf_silu_kernel(
             nc.sync.dma_start(out=wh4_sc[r:P:32, :], in_=wh4_scales[0, r:16:4, :].bitcast(I32))
         load_rec(0)
         load_wg(0)
+        load_rec(1)
         nc.sync.dma_start(out=bias_rows[0:4, :], in_=bg.rearrange("(c p) -> c p", p=P))
         for r in range(4):
             nc.sync.dma_start(
                 out=wg_sc[r:P:32], in_=wg_scales[:, r:16:4, :].rearrange("a q t -> q a t").bitcast(I32)
             )
-        load_rec(1)
         load_wg(1)
         load_rec(2)
         load_rec(3)
@@ -258,23 +258,22 @@ def tile_list_hwayt_qf_silu_kernel(
         for c in range(2):
             for h in range(2):
                 differ(c, cols(h))
+        hidden_close(2, whole, J, hidden_open(2, whole, "b6"))
         gate(0, "b4")
         gate(1, "b5")
-        hidden_close(2, whole, J, hidden_open(2, whole, "b4"))
-        hidden_close(3, whole, J, hidden_open(3, whole, "b5"))
+        hidden_close(3, whole, J, hidden_open(3, whole, "b4"))
         gate(2, "b0")
+        gate(3, "b1")
         weigh(0, whole, "part0")
         weigh(1, whole, "part1")
-        sum_close(1, sum_open(1, "b4"))
-        gate(3, "b5")
+        finish(0, whole, nc.sync)
+        sum_close(1, sum_open(1, "b5"))
         turn_back(1, "b2")
         differ(2, whole)
-        finish(0, whole, nc.sync)
+        differ(3, whole)
         weigh(2, whole, "part2")
-        differ(3, cols(0))
-        finish(2, whole, nc.sync)
-        differ(3, cols(1))
         weigh(3, cols(0), "part3")
+        finish(2, whole, nc.sync)
         weigh(3, cols(1), "turned0")
         res.append(sb.tile([P, J], F32, name="res3", tag="turned1"))
         finish(3, cols(0), nc.sync)

@@ -118,9 +118,9 @@ def tile_list_hwayt_qf_silu_kernel(
         def gather_scales(a, js):
             nc.vector.tensor_copy(out=got_sc[:, a, js], in_=tab_sc[:, a, :].bitcast(U8).indirect(offs_of(js)))
 
-        def round_wh8(c):
+        def round_wh8(c, copy=nc.scalar.copy):
             u, m = min(c, 1), max(c - 1, 0)
-            nc.scalar.copy(
+            copy(
                 out=grouped[c][:].rearrange("p (g m) i -> p g i m", m=4),
                 in_=raw[u][:, :, m * P : (m + 1) * P].rearrange("p i (g m) -> p g i m", m=4),
             )
@@ -243,7 +243,7 @@ def tile_list_hwayt_qf_silu_kernel(
             gather_scales(h, cols(h))
             gather_scales(1 - h, cols(h))
         round_wh8(2)
-        round_wh8(3)
+        round_wh8(3, nc.gpsimd.tensor_copy)
         quantize_wh8(1)
         quantize_wh8(2)
         quantize_wh8(3)

@@ -45,12 +45,12 @@ def tile_list_hwayt_qf_silu_kernel(
         grouped = [sb.tile([P, P, 4], BF16, name="grouped%d" % c, align_bytes=64) for c in range(4)]
         wh8_w = [sb.tile([P, P], U32, name="wh8_w%d" % c, align_bytes=64) for c in range(4)]
         wh8_sc = [sb.tile([P, P], U8, name="wh8_sc%d" % c, align_bytes=64) for c in range(4)]
-        rec = [sb.tile([P, T], F32, name="rec%d" % c, align_bytes=64) for c in range(4)]
+        rec = [sb.tile([P, T], F32, name="rec", tag="rec%d" % c, align_bytes=64) for c in range(4)]
         got_w = sb.tile([P, J], U32, name="got_w", align_bytes=64)
         got_sc = sb.tile([P, 2, J], U8, name="got_sc", align_bytes=64)
         item_w = sb.tile([P, 2, J], U16, name="item_w", align_bytes=64)
         lean = [sb.tile([P, J], F32, name="lean%d" % c) for c in range(4)]
-        act = [sb.tile([P, J], F32, name="act%d" % c) for c in range(4)]
+        act = [sb.tile([P, J], F32, name="act", tag="act%d" % c) for c in range(4)]
         diff = {}
         part = {}
         res = [sb.tile([P, J], F32, name="res%d" % c) for c in range(3)]
@@ -91,21 +91,17 @@ def tile_list_hwayt_qf_silu_kernel(
         nc.sync.dma_start(out=wh4_w[:], in_=wh4_words[0].bitcast(I32))
         for r in range(4):
             nc.sync.dma_start(out=wh4_sc[r:P:32, :], in_=wh4_scales[0, r:16:4, :].bitcast(I32))
-        load_rec(0)
-        load_wg(0)
-        load_rec(1)
         nc.sync.dma_start(out=bias_rows[0:4, :], in_=bg.rearrange("(c p) -> c p", p=P))
+        load_rec(0)
+        load_rec(1)
+        load_wg(0)
         for r in range(4):
             nc.sync.dma_start(
                 out=wg_sc[r:P:32], in_=wg_scales[:, r:16:4, :].rearrange("a q t -> q a t").bitcast(I32)
             )
-        load_wg(1)
         load_rec(2)
+        load_wg(1)
         load_rec(3)
-
-        bias_cols = ps.tile([P, P], F32, name="bias_cols", tag="b7")
-        nc.tensor.transpose(bias_cols[:], bias_rows[:], ident[:])
-        nc.scalar.activation(out=half_bias[:], in_=bias_cols[:, 0:4], func=ACT.Identity, scale=-0.5, bias=zero[:])
 
         def cols(h):
             return slice(h * HALF, (h + 1) * HALF)
@@ -184,20 +180,20 @@ def tile_list_hwayt_qf_silu_kernel(
 
         def differ(c, js):
             if c not in diff:
-                diff[c] = sb.tile([P, J], F32, name="diff", tag="diff%d" % (c % 2))
+                diff[c] = sb.tile([P, J], F32, name="diff", tag=["diff0", "diff1", "diff2", "act0"][c])
             nc.vector.tensor_tensor(
                 out=diff[c][:, js], in0=rec[c][:].indirect(offs_of(js)), in1=act[c][:, js], op=ALU.subtract
             )
 
-        def weigh(c, js, tag):
-            part[c, js.start] = sb.tile([P, js.stop - js.start], F32, name="part", tag=tag)
+        def weigh(c, js, dst):
+            part[c, js.start] = dst
             nc.vector.scalar_tensor_tensor(
-                out=part[c, js.start][:], in0=lean[c][:, js], scalar=1.0, in1=diff[c][:, js], op0=ALU.add, op1=ALU.mult
+                out=part[c, js.start], in0=lean[c][:, js], scalar=1.0, in1=diff[c][:, js], op0=ALU.add, op1=ALU.mult
             )
 
         def finish(c, js, queue):
             nc.vector.scalar_tensor_tensor(
-                out=res[c][:, js], in0=part[c, js.start][:], scalar=0.5, in1=act[c][:, js], op0=ALU.mult, op1=ALU.add
+                out=res[c][:, js], in0=part[c, js.start], scalar=0.5, in1=act[c][:, js], op0=ALU.mult, op1=ALU.add
             )
             queue.dma_start(out=out[c * P : (c + 1) * P, js], in_=res[c][:, js])
 
@@ -259,22 +255,27 @@ def tile_list_hwayt_qf_silu_kernel(
             for h in range(2):
                 differ(c, cols(h))
         hidden_close(2, whole, J, hidden_open(2, whole, "b6"))
+        differ(2, whole)
+        bias_cols = ps.tile([P, P], F32, name="bias_cols", tag="b3")
+        nc.tensor.transpose(bias_cols[:], bias_rows[:], ident[:])
+        nc.scalar.activation(out=half_bias[:], in_=bias_cols[:, 0:4], func=ACT.Identity, scale=-0.5, bias=zero[:])
         gate(0, "b4")
         gate(1, "b5")
         hidden_close(3, whole, J, hidden_open(3, whole, "b4"))
         gate(2, "b0")
         gate(3, "b1")
-        weigh(0, whole, "part0")
-        weigh(1, whole, "part1")
+        parts = sb.tile([P, 2 * J], F32, name="parts", tag="rec2", align_bytes=64)
+        weigh(0, whole, parts[:, 0:J])
+        weigh(1, whole, parts[:, J : 2 * J])
+        weigh(2, whole, sb.tile([P, J], F32, name="part2")[:])
         finish(0, whole, nc.sync)
+        finish(2, whole, nc.sync)
         sum_close(1, sum_open(1, "b5"))
         turn_back(1, "b2")
-        differ(2, whole)
-        differ(3, whole)
-        weigh(2, whole, "part2")
-        weigh(3, cols(0), "part3")
-        finish(2, whole, nc.sync)
-        weigh(3, cols(1), "turned0")
-        res.append(sb.tile([P, J], F32, name="res3", tag="turned1"))
-        finish(3, cols(0), nc.sync)
-        finish(3, cols(1), nc.scalar)
+        for h in range(2):
+            differ(3, cols(h))
+        for h in range(2):
+            weigh(3, cols(h), sb.tile([P, HALF], F32, name="part3%d" % h)[:])
+        res.append(sb.tile([P, J], F32, name="res3"))
+        for h in range(2):
+            finish(3, cols(h), nc.sync)

@@ -41,34 +41,27 @@ def tile_list_hwayt_qf_silu_kernel(
         half_bias = sb.tile([P, 4], F32, name="half_bias")
         zero_in = sb.tile([P, 1], F32, name="zero_in")
         zero = sb.tile([P, 1], F32, name="zero")
-        raw = [sb.tile([P, 4, w], F32, name="raw%d" % w, align_bytes=64) for w in (P, N - P)]
-        grouped = [sb.tile([P, P, 4], BF16, name="grouped%d" % c, align_bytes=64) for c in range(4)]
+        raw = sb.tile([P, 4, N], F32, name="raw", align_bytes=64)
+        grouped = [sb.tile([P, P, 4], BF16, name="grouped", tag="grouped%d" % c, align_bytes=64) for c in range(4)]
         wh8_w = [sb.tile([P, P], U32, name="wh8_w%d" % c, align_bytes=64) for c in range(4)]
         wh8_sc = [sb.tile([P, P], U8, name="wh8_sc%d" % c, align_bytes=64) for c in range(4)]
         rec = [sb.tile([P, T], F32, name="rec", tag="rec%d" % c, align_bytes=64) for c in range(4)]
         got_w = sb.tile([P, J], U32, name="got_w", align_bytes=64)
-        got_sc = sb.tile([P, 2, J], U8, name="got_sc", align_bytes=64)
         item_w = sb.tile([P, 2, J], U16, name="item_w", align_bytes=64)
         lean = [sb.tile([P, J], F32, name="lean%d" % c) for c in range(4)]
         act = [sb.tile([P, J], F32, name="act", tag="act%d" % c) for c in range(4)]
         diff = {}
         part = {}
-        res = [sb.tile([P, J], F32, name="res%d" % c) for c in range(3)]
-        turned = [sb.tile([P, 2, P], F32, name="turned", tag="turned%d" % h) for h in range(2)]
-        item_sc = [got_sc[:, 0, :], got_sc[:, 1, :]]
+        res = [sb.tile([P, J], F32, name="res%d" % c) for c in range(4)]
+        turned = [sb.tile([P, 4, P], F32, name="turned%d" % c) for c in range(2)]
+        item_sc = {}
 
-        nc.vector.memset(tab_sc[:], 0)
+        nc.gpsimd.memset(tab_sc[:], 0)
         nc.vector.memset(wh4_sc[:], 0)
         nc.vector.memset(wg_sc[:], 0)
         nc.gpsimd.memset(bias_rows[:], 0.0)
         nc.gpsimd.memset(zero_in[:], 0.0)
         make_identity(nc, ident[:])
-
-        def load_wh8(u):
-            nc.sync.dma_start(
-                out=raw[u][:],
-                in_=wh8[:, u * P : P + u * (N - P)].rearrange("(p i) n -> p i n", i=4),
-            )
 
         def load_wg(u):
             nc.sync.dma_start(
@@ -81,25 +74,24 @@ def tile_list_hwayt_qf_silu_kernel(
 
         nc.sync.dma_start(out=tab_w[:], in_=tab_words[0].rearrange("p t b -> p (t b)").bitcast(I32))
         nc.sync.dma_start(offsets[:], offs)
-        load_wh8(0)
         for r in range(4):
             nc.sync.dma_start(
                 out=tab_sc[r:P:32], in_=tab_scales[:, r:16:4, :].rearrange("a q t -> q a t").bitcast(I32)
             )
         nc.scalar.activation(out=zero[:], in_=zero_in[:], func=ACT.Silu)
-        load_wh8(1)
+        nc.sync.dma_start(out=raw[:], in_=wh8.rearrange("(p i) n -> p i n", i=4))
         nc.sync.dma_start(out=wh4_w[:], in_=wh4_words[0].bitcast(I32))
         for r in range(4):
             nc.sync.dma_start(out=wh4_sc[r:P:32, :], in_=wh4_scales[0, r:16:4, :].bitcast(I32))
-        nc.sync.dma_start(out=bias_rows[0:4, :], in_=bg.rearrange("(c p) -> c p", p=P))
         load_rec(0)
         load_rec(1)
         load_wg(0)
+        nc.sync.dma_start(out=bias_rows[0:4, :], in_=bg.rearrange("(c p) -> c p", p=P))
+        load_rec(2)
         for r in range(4):
             nc.sync.dma_start(
                 out=wg_sc[r:P:32], in_=wg_scales[:, r:16:4, :].rearrange("a q t -> q a t").bitcast(I32)
             )
-        load_rec(2)
         load_wg(1)
         load_rec(3)
 
@@ -111,14 +103,19 @@ def tile_list_hwayt_qf_silu_kernel(
         def offs_of(js):
             return offsets[:, js.start // 16 : js.stop // 16]
 
-        def gather_scales(a, js):
-            nc.vector.tensor_copy(out=got_sc[:, a, js], in_=tab_sc[:, a, :].bitcast(U8).indirect(offs_of(js)))
+        def gather_scales(a, js, tag):
+            got = sb.tile([P, js.stop - js.start], U8, name="got_sc", tag=tag, align_bytes=64)
+            for h in range(js.start // HALF, js.stop // HALF):
+                item_sc[a, h] = got[:, h * HALF - js.start : (h + 1) * HALF - js.start]
+            nc.vector.tensor_copy(out=got[:], in_=tab_sc[:, a, :].bitcast(U8).indirect(offs_of(js)))
+
+        def round_on_gpsimd(out, in_):
+            nc.gpsimd.tensor_scalar(out=out, in0=in_, scalar1=1.0, scalar2=0.0, op0=ALU.mult, op1=ALU.add)
 
         def round_wh8(c, copy=nc.scalar.copy):
-            u, m = min(c, 1), max(c - 1, 0)
             copy(
                 out=grouped[c][:].rearrange("p (g m) i -> p g i m", m=4),
-                in_=raw[u][:, :, m * P : (m + 1) * P].rearrange("p i (g m) -> p g i m", m=4),
+                in_=raw[:, :, c * P : (c + 1) * P].rearrange("p i (g m) -> p g i m", m=4),
             )
 
         def quantize_wh8(c):
@@ -130,57 +127,59 @@ def tile_list_hwayt_qf_silu_kernel(
 
         def gate(c, tag):
             acc = ps.tile([P, J], F32, name="ga", tag=tag)
-            for a in range(2):
+            for a, h in ((0, 0), (0, 1), (1, 0), (1, 1)):
                 nc.tensor.matmul_mx(
-                    out=acc[:],
+                    out=acc[:, cols(h)],
                     lhsT=wg_w[c // 2][:, a, (c % 2) * P : (c % 2 + 1) * P].bitcast(FP8X4),
                     lhsT_scale=wg_sc[:, a, c * 32 : (c + 1) * 32].bitcast(U8),
-                    rhs=item_w[:, a, :].bitcast(FP4X4),
-                    rhs_scale=item_sc[a],
-                    start=(a == 0),
-                    stop=(a == 1),
+                    rhs=item_w[:, a, cols(h)].bitcast(FP4X4),
+                    rhs_scale=item_sc[a, h],
+                    start=(a == 0 and h == 0),
+                    stop=(a == 1 and h == 1),
                 )
             nc.scalar.activation(out=lean[c][:], in_=acc[:], func=ACT.Tanh, bias=half_bias[:, c : c + 1], scale=-0.5)
 
-        def wh4_pass(c, js, acc, start, stop):
+        def wh4_pass(c, h, acc, start, stop):
             nc.tensor.matmul_mx(
-                out=acc[:],
+                out=acc,
                 lhsT=wh4_w[:, c * 64 : (c + 1) * 64].bitcast(FP4X4),
                 lhsT_scale=wh4_sc[:, c * 32 : (c + 1) * 32].bitcast(U8),
-                rhs=item_w[:, 1, js].bitcast(FP4X4),
-                rhs_scale=item_sc[1][:, js],
+                rhs=item_w[:, 1, cols(h)].bitcast(FP4X4),
+                rhs_scale=item_sc[1, h],
                 start=start,
                 stop=stop,
             )
 
-        def wh8_pass(c, js, step, acc, start, stop):
-            width = js.stop - js.start
-            for s in range(0, width, step):
-                nc.tensor.matmul_mx(
-                    out=acc[:, s : s + step],
-                    lhsT=wh8_w[c][:].bitcast(FP8X4),
-                    lhsT_scale=wh8_sc[c][:],
-                    rhs=item_w[:, 0, js.start + s : js.start + s + step].bitcast(FP4X4),
-                    rhs_scale=item_sc[0][:, js.start + s : js.start + s + step],
-                    start=(start and s == 0),
-                    stop=(stop and s + step == width),
-                )
+        def wh8_pass(c, h, acc, start, stop):
+            nc.tensor.matmul_mx(
+                out=acc,
+                lhsT=wh8_w[c][:].bitcast(FP8X4),
+                lhsT_scale=wh8_sc[c][:],
+                rhs=item_w[:, 0, cols(h)].bitcast(FP4X4),
+                rhs_scale=item_sc[0, h],
+                start=start,
+                stop=stop,
+            )
 
-        def silu(c, js, acc):
-            nc.scalar.activation(out=act[c][:, js], in_=acc[:], func=ACT.Silu)
-
-        def hidden_open(c, js, tag):
-            acc = ps.tile([P, js.stop - js.start], F32, name="ha", tag=tag)
-            wh4_pass(c, js, acc, True, False)
+        def hidden_open(c, halves, tag):
+            acc = ps.tile([P, len(halves), HALF], F32, name="ha", tag=tag)
+            wh4_pass(c, halves[0], acc[:, 0, :], True, False)
             return acc
 
-        def hidden_close(c, js, step, acc):
-            wh8_pass(c, js, step, acc, False, True)
-            silu(c, js, acc)
+        def hidden_close(c, halves, acc):
+            for n, h in enumerate(halves):
+                wh8_pass(c, h, acc[:, n, :], False, h == halves[-1])
+            js = slice(halves[0] * HALF, (halves[-1] + 1) * HALF)
+            nc.scalar.activation(out=act[c][:, js], in_=acc[:].rearrange("p n j -> p (n j)"), func=ACT.Silu)
+
+        def hidden(c, tag):
+            acc = hidden_open(c, (0, 1), tag)
+            wh4_pass(c, 1, acc[:, 1, :], False, False)
+            hidden_close(c, (0, 1), acc)
 
         def differ(c, js):
             if c not in diff:
-                diff[c] = sb.tile([P, J], F32, name="diff", tag=["diff0", "diff1", "diff2", "act0"][c])
+                diff[c] = sb.tile([P, J], F32, name="diff", tag="diff%d" % c)
             nc.vector.tensor_tensor(
                 out=diff[c][:, js], in0=rec[c][:].indirect(offs_of(js)), in1=act[c][:, js], op=ALU.subtract
             )
@@ -191,40 +190,43 @@ def tile_list_hwayt_qf_silu_kernel(
                 out=part[c, js.start], in0=lean[c][:, js], scalar=1.0, in1=diff[c][:, js], op0=ALU.add, op1=ALU.mult
             )
 
-        def finish(c, js, queue):
+        def finish(c, js):
             nc.vector.scalar_tensor_tensor(
                 out=res[c][:, js], in0=part[c, js.start], scalar=0.5, in1=act[c][:, js], op0=ALU.mult, op1=ALU.add
             )
-            queue.dma_start(out=out[c * P : (c + 1) * P, js], in_=res[c][:, js])
+
+        def store(c, js):
+            nc.sync.dma_start(out=out[c * P : (c + 1) * P, js], in_=res[c][:, js])
 
         def add_turned(acc, term, start, stop):
-            for b in range(4):
+            blocks = acc.shape[1]
+            for b in range(blocks):
                 nc.tensor.matmul(
                     acc[:, b, :],
                     term[:, b * P : (b + 1) * P],
                     ident[:],
                     is_transpose=True,
                     start=(start and b == 0),
-                    stop=(stop and b == 3),
+                    stop=(stop and b == blocks - 1),
                 )
 
-        def sum_open(c, tag):
-            acc = ps.tile([P, 4, P], F32, name="sum", tag=tag)
+        def sum_open(c, blocks, tag):
+            acc = ps.tile([P, blocks, P], F32, name="sum", tag=tag)
             add_turned(acc, act[c], True, False)
             add_turned(acc, act[c], False, False)
             return acc
 
         def sum_close(c, acc):
             add_turned(acc, part[c, 0], False, True)
-            for h in range(2):
-                nc.scalar.activation(out=turned[h][:], in_=acc[:, 2 * h : 2 * h + 2, :], func=ACT.Copy, scale=0.5)
+            nc.scalar.activation(out=turned[c][:, 0 : acc.shape[1], :], in_=acc[:], func=ACT.Copy, scale=0.5)
 
-        def turn_back(c, tag):
-            acc = ps.tile([P, 4, P], F32, name="back", tag=tag)
-            for b in range(4):
-                nc.tensor.transpose(acc[:, b, :], turned[b // 2][:, b % 2, :], ident[:])
-            nc.scalar.copy(out=res[c][:], in_=acc[:].rearrange("p b j -> p (b j)"))
-            nc.scalar.dma_start(out=out[c * P : (c + 1) * P, :], in_=res[c][:])
+        def turn_back(c, blocks, tag):
+            acc = ps.tile([P, blocks, P], F32, name="back", tag=tag)
+            js = slice(0, blocks * P)
+            for b in range(blocks):
+                nc.tensor.transpose(acc[:, b, :], turned[c][:, b, :], ident[:])
+            nc.scalar.copy(out=res[c][:, js], in_=acc[:].rearrange("p b j -> p (b j)"))
+            nc.scalar.dma_start(out=out[c * P : (c + 1) * P, js], in_=res[c][:, js])
 
         round_wh8(0)
         round_wh8(1)
@@ -234,48 +236,52 @@ def tile_list_hwayt_qf_silu_kernel(
             nc.vector.tensor_copy(
                 out=item_w[:, :, cols(h)], in_=got_w[:, cols(h)].bitcast(U16).rearrange("p (j d) -> p d j", d=2)
             )
+        gather_scales(1, whole, "sc1")
+        gather_scales(0, cols(0), "sc0")
         quantize_wh8(0)
-        for h in range(2):
-            gather_scales(h, cols(h))
-            gather_scales(1 - h, cols(h))
+        gather_scales(0, cols(1), "grouped0")
         round_wh8(2)
-        round_wh8(3, nc.gpsimd.tensor_copy)
+        round_wh8(3, round_on_gpsimd)
         quantize_wh8(1)
         quantize_wh8(2)
         quantize_wh8(3)
-        first = ps.tile([P, HALF], F32, name="ha", tag="b0")
-        wh8_pass(0, cols(0), P, first, True, False)
-        wh4_pass(0, cols(0), first, False, True)
-        silu(0, cols(0), first)
-        opened = [hidden_open(c, cols(h), "b%d" % (c + 2 * h)) for c, h in ((1, 0), (0, 1), (1, 1))]
-        hidden_close(0, cols(1), P, opened[1])
-        hidden_close(1, cols(0), P, opened[0])
-        hidden_close(1, cols(1), P, opened[2])
-        for c in range(2):
-            for h in range(2):
-                differ(c, cols(h))
-        hidden_close(2, whole, J, hidden_open(2, whole, "b6"))
+        tile0 = [hidden_open(0, (h,), "b%d" % h) for h in range(2)]
+        hidden_close(0, (0,), tile0[0])
+        tile1 = hidden_open(1, (0, 1), "b2")
+        wh4_pass(1, 1, tile1[:, 1, :], False, False)
+        hidden_close(0, (1,), tile0[1])
+        hidden_close(1, (0, 1), tile1)
+        for h in range(2):
+            differ(0, cols(h))
+        differ(1, whole)
+        hidden(2, "b6")
+        hidden(3, "b7")
         differ(2, whole)
         bias_cols = ps.tile([P, P], F32, name="bias_cols", tag="b3")
         nc.tensor.transpose(bias_cols[:], bias_rows[:], ident[:])
-        nc.scalar.activation(out=half_bias[:], in_=bias_cols[:, 0:4], func=ACT.Identity, scale=-0.5, bias=zero[:])
+        nc.vector.tensor_scalar(
+            out=half_bias[:], in0=bias_cols[:, 0:4], scalar1=-0.5, scalar2=zero[:], op0=ALU.mult, op1=ALU.add
+        )
         gate(0, "b4")
         gate(1, "b5")
-        hidden_close(3, whole, J, hidden_open(3, whole, "b4"))
         gate(2, "b0")
         gate(3, "b1")
-        parts = sb.tile([P, 2 * J], F32, name="parts", tag="rec2", align_bytes=64)
-        weigh(0, whole, parts[:, 0:J])
-        weigh(1, whole, parts[:, J : 2 * J])
-        weigh(2, whole, sb.tile([P, J], F32, name="part2")[:])
-        finish(0, whole, nc.sync)
-        finish(2, whole, nc.sync)
-        sum_close(1, sum_open(1, "b5"))
-        turn_back(1, "b2")
+        weigh(0, whole, sb.tile([P, J], F32, name="part0")[:])
+        for c, h in ((1, 1), (1, 0), (2, 0), (2, 1)):
+            weigh(c, cols(h), sb.tile([P, HALF], F32, name="part%d%d" % (c, h))[:])
+        sum_close(0, sum_open(0, 4, "b4"))
+        sum_close(1, sum_open(1, 2, "b5"))
+        turn_back(0, 4, "b2")
+        turn_back(1, 2, "b6")
+        finish(1, cols(1))
+        store(1, cols(1))
+        for h in range(2):
+            finish(2, cols(h))
+        store(2, whole)
         for h in range(2):
             differ(3, cols(h))
         for h in range(2):
             weigh(3, cols(h), sb.tile([P, HALF], F32, name="part3%d" % h)[:])
-        res.append(sb.tile([P, J], F32, name="res3"))
         for h in range(2):
-            finish(3, cols(h), nc.sync)
+            finish(3, cols(h))
+            store(3, cols(h))

from contextlib import ExitStack

import concourse.mybir as mybir
from concourse.masks import make_identity

K, N, T, J = 1024, 512, 1024, 512
FLOPS = 2 * 2 * K * N * J

F32 = mybir.dt.float32
BF16 = mybir.dt.bfloat16
I32 = mybir.dt.int32
U32 = mybir.dt.uint32
U16 = mybir.dt.uint16
U8 = mybir.dt.uint8
FP8X4 = mybir.dt.float8_e4m3fn_x4
FP4X4 = mybir.dt.float4_e2m1fn_x4
ACT = mybir.ActivationFunctionType
ALU = mybir.AluOpType

P = 128
HALF = J // 2


def tile_list_hwayt_qf_silu_kernel(
    tc, tab_words, tab_scales, wg_words, wg_scales, wh8, wh4_words, wh4_scales, bg, rT, offs, out
):
    nc = tc.nc
    with ExitStack() as ctx:
        sb = ctx.enter_context(tc.tile_pool(name="sb", bufs=1))
        ps = ctx.enter_context(tc.psum_pool(name="ps", bufs=1))

        offsets = sb.tile([P, J // 16], U16, name="offsets")
        tab_sc = sb.tile([P, 2, T // 4], I32, name="tab_sc", align_bytes=64)
        tab_w = sb.tile([P, T], I32, name="tab_w", align_bytes=64)
        wg_sc = sb.tile([P, 2, N // 4], I32, name="wg_sc", align_bytes=64)
        wg_w = [sb.tile([P, 2, N // 2], I32, name="wg_w%d" % u, align_bytes=64) for u in range(2)]
        wh4_sc = sb.tile([P, N // 4], I32, name="wh4_sc", align_bytes=64)
        wh4_w = sb.tile([P, N // 2], I32, name="wh4_w", align_bytes=64)
        bias_rows = sb.tile([P, P], F32, name="bias_rows")
        ident = sb.tile([P, P], F32, name="ident")
        half_bias = sb.tile([P, 4], F32, name="half_bias")
        zero_in = sb.tile([P, 1], F32, name="zero_in")
        zero = sb.tile([P, 1], F32, name="zero")
        raw = sb.tile([P, 4, N], F32, name="raw", align_bytes=64)
        grouped = [sb.tile([P, P, 4], BF16, name="grouped", tag="grouped%d" % c, align_bytes=64) for c in range(4)]
        wh8_w = [sb.tile([P, P], U32, name="wh8_w%d" % c, align_bytes=64) for c in range(4)]
        wh8_sc = [sb.tile([P, P], U8, name="wh8_sc%d" % c, align_bytes=64) for c in range(4)]
        rec = [sb.tile([P, T], F32, name="rec", tag="rec%d" % c, align_bytes=64) for c in range(4)]
        got_w = sb.tile([P, J], U32, name="got_w", align_bytes=64)
        item_w = sb.tile([P, 2, J], U16, name="item_w", align_bytes=64)
        lean = [sb.tile([P, J], F32, name="lean%d" % c) for c in range(4)]
        act = [sb.tile([P, J], F32, name="act", tag="act%d" % c) for c in range(4)]
        diff = {}
        part = {}
        res = [sb.tile([P, J], F32, name="res%d" % c) for c in range(4)]
        turned = [sb.tile([P, 4, P], F32, name="turned%d" % c) for c in range(2)]
        item_sc = {}

        nc.gpsimd.memset(tab_sc[:], 0)
        nc.vector.memset(wh4_sc[:], 0)
        nc.vector.memset(wg_sc[:], 0)
        nc.gpsimd.memset(bias_rows[:], 0.0)
        nc.gpsimd.memset(zero_in[:], 0.0)
        make_identity(nc, ident[:])

        def load_wg(u):
            nc.sync.dma_start(
                out=wg_w[u][:],
                in_=wg_words[:, :, u * 256 : (u + 1) * 256, :].rearrange("a p n i -> p a (n i)").bitcast(I32),
            )

        def load_rec(c):
            nc.sync.dma_start(out=rec[c][:], in_=rT[c * P : (c + 1) * P, :])

        nc.sync.dma_start(out=tab_w[:], in_=tab_words[0].rearrange("p t b -> p (t b)").bitcast(I32))
        nc.sync.dma_start(offsets[:], offs)
        for r in range(4):
            nc.sync.dma_start(
                out=tab_sc[r:P:32], in_=tab_scales[:, r:16:4, :].rearrange("a q t -> q a t").bitcast(I32)
            )
        nc.scalar.activation(out=zero[:], in_=zero_in[:], func=ACT.Silu)
        nc.sync.dma_start(out=raw[:], in_=wh8.rearrange("(p i) n -> p i n", i=4))
        nc.sync.dma_start(out=wh4_w[:], in_=wh4_words[0].bitcast(I32))
        for r in range(4):
            nc.sync.dma_start(out=wh4_sc[r:P:32, :], in_=wh4_scales[0, r:16:4, :].bitcast(I32))
        load_rec(0)
        load_rec(1)
        load_wg(0)
        nc.sync.dma_start(out=bias_rows[0:4, :], in_=bg.rearrange("(c p) -> c p", p=P))
        load_rec(2)
        for r in range(4):
            nc.sync.dma_start(
                out=wg_sc[r:P:32], in_=wg_scales[:, r:16:4, :].rearrange("a q t -> q a t").bitcast(I32)
            )
        load_wg(1)
        load_rec(3)

        def cols(h):
            return slice(h * HALF, (h + 1) * HALF)

        whole = slice(0, J)

        def offs_of(js):
            return offsets[:, js.start // 16 : js.stop // 16]

        def gather_scales(a, js, tag):
            got = sb.tile([P, js.stop - js.start], U8, name="got_sc", tag=tag, align_bytes=64)
            for h in range(js.start // HALF, js.stop // HALF):
                item_sc[a, h] = got[:, h * HALF - js.start : (h + 1) * HALF - js.start]
            nc.vector.tensor_copy(out=got[:], in_=tab_sc[:, a, :].bitcast(U8).indirect(offs_of(js)))

        def round_on_gpsimd(out, in_):
            nc.gpsimd.tensor_scalar(out=out, in0=in_, scalar1=1.0, scalar2=0.0, op0=ALU.mult, op1=ALU.add)

        def round_wh8(c, copy=nc.scalar.copy):
            copy(
                out=grouped[c][:].rearrange("p (g m) i -> p g i m", m=4),
                in_=raw[:, :, c * P : (c + 1) * P].rearrange("p i (g m) -> p g i m", m=4),
            )

        def quantize_wh8(c):
            nc.vector.quantize_mx(
                out=wh8_w[c][:].bitcast(FP8X4),
                scales=wh8_sc[c][:],
                in_=grouped[c][:].rearrange("p n i -> p (n i)"),
            )

        def gate(c, tag):
            acc = ps.tile([P, J], F32, name="ga", tag=tag)
            for a, h in ((0, 0), (0, 1), (1, 0), (1, 1)):
                nc.tensor.matmul_mx(
                    out=acc[:, cols(h)],
                    lhsT=wg_w[c // 2][:, a, (c % 2) * P : (c % 2 + 1) * P].bitcast(FP8X4),
                    lhsT_scale=wg_sc[:, a, c * 32 : (c + 1) * 32].bitcast(U8),
                    rhs=item_w[:, a, cols(h)].bitcast(FP4X4),
                    rhs_scale=item_sc[a, h],
                    start=(a == 0 and h == 0),
                    stop=(a == 1 and h == 1),
                )
            nc.scalar.activation(out=lean[c][:], in_=acc[:], func=ACT.Tanh, bias=half_bias[:, c : c + 1], scale=-0.5)

        def wh4_pass(c, h, acc, start, stop):
            nc.tensor.matmul_mx(
                out=acc,
                lhsT=wh4_w[:, c * 64 : (c + 1) * 64].bitcast(FP4X4),
                lhsT_scale=wh4_sc[:, c * 32 : (c + 1) * 32].bitcast(U8),
                rhs=item_w[:, 1, cols(h)].bitcast(FP4X4),
                rhs_scale=item_sc[1, h],
                start=start,
                stop=stop,
            )

        def wh8_pass(c, h, acc, start, stop):
            nc.tensor.matmul_mx(
                out=acc,
                lhsT=wh8_w[c][:].bitcast(FP8X4),
                lhsT_scale=wh8_sc[c][:],
                rhs=item_w[:, 0, cols(h)].bitcast(FP4X4),
                rhs_scale=item_sc[0, h],
                start=start,
                stop=stop,
            )

        def hidden_open(c, halves, tag):
            acc = ps.tile([P, len(halves), HALF], F32, name="ha", tag=tag)
            wh4_pass(c, halves[0], acc[:, 0, :], True, False)
            return acc

        def hidden_close(c, halves, acc):
            for n, h in enumerate(halves):
                wh8_pass(c, h, acc[:, n, :], False, h == halves[-1])
            js = slice(halves[0] * HALF, (halves[-1] + 1) * HALF)
            nc.scalar.activation(out=act[c][:, js], in_=acc[:].rearrange("p n j -> p (n j)"), func=ACT.Silu)

        def hidden(c, tag):
            acc = hidden_open(c, (0, 1), tag)
            wh4_pass(c, 1, acc[:, 1, :], False, False)
            hidden_close(c, (0, 1), acc)

        def differ(c, js):
            if c not in diff:
                diff[c] = sb.tile([P, J], F32, name="diff", tag="diff%d" % c)
            nc.vector.tensor_tensor(
                out=diff[c][:, js], in0=rec[c][:].indirect(offs_of(js)), in1=act[c][:, js], op=ALU.subtract
            )

        def weigh(c, js, dst):
            part[c, js.start] = dst
            nc.vector.scalar_tensor_tensor(
                out=part[c, js.start], in0=lean[c][:, js], scalar=1.0, in1=diff[c][:, js], op0=ALU.add, op1=ALU.mult
            )

        def finish(c, js):
            nc.vector.scalar_tensor_tensor(
                out=res[c][:, js], in0=part[c, js.start], scalar=0.5, in1=act[c][:, js], op0=ALU.mult, op1=ALU.add
            )

        def store(c, js):
            nc.sync.dma_start(out=out[c * P : (c + 1) * P, js], in_=res[c][:, js])

        def add_turned(acc, term, start, stop):
            blocks = acc.shape[1]
            for b in range(blocks):
                nc.tensor.matmul(
                    acc[:, b, :],
                    term[:, b * P : (b + 1) * P],
                    ident[:],
                    is_transpose=True,
                    start=(start and b == 0),
                    stop=(stop and b == blocks - 1),
                )

        def sum_open(c, blocks, tag):
            acc = ps.tile([P, blocks, P], F32, name="sum", tag=tag)
            add_turned(acc, act[c], True, False)
            add_turned(acc, act[c], False, False)
            return acc

        def sum_close(c, acc):
            add_turned(acc, part[c, 0], False, True)
            nc.scalar.activation(out=turned[c][:, 0 : acc.shape[1], :], in_=acc[:], func=ACT.Copy, scale=0.5)

        def turn_back(c, blocks, tag):
            acc = ps.tile([P, blocks, P], F32, name="back", tag=tag)
            js = slice(0, blocks * P)
            for b in range(blocks):
                nc.tensor.transpose(acc[:, b, :], turned[c][:, b, :], ident[:])
            nc.scalar.copy(out=res[c][:, js], in_=acc[:].rearrange("p b j -> p (b j)"))
            nc.scalar.dma_start(out=out[c * P : (c + 1) * P, js], in_=res[c][:, js])

        round_wh8(0)
        round_wh8(1)
        for h in range(2):
            nc.vector.tensor_copy(out=got_w[:, cols(h)], in_=tab_w[:].bitcast(U32).indirect(offs_of(cols(h))))
        for h in range(2):
            nc.vector.tensor_copy(
                out=item_w[:, :, cols(h)], in_=got_w[:, cols(h)].bitcast(U16).rearrange("p (j d) -> p d j", d=2)
            )
        gather_scales(1, whole, "sc1")
        gather_scales(0, cols(0), "sc0")
        quantize_wh8(0)
        gather_scales(0, cols(1), "grouped0")
        round_wh8(2)
        round_wh8(3, round_on_gpsimd)
        quantize_wh8(1)
        quantize_wh8(2)
        quantize_wh8(3)
        tile0 = [hidden_open(0, (h,), "b%d" % h) for h in range(2)]
        hidden_close(0, (0,), tile0[0])
        tile1 = hidden_open(1, (0, 1), "b2")
        wh4_pass(1, 1, tile1[:, 1, :], False, False)
        hidden_close(0, (1,), tile0[1])
        hidden_close(1, (0, 1), tile1)
        for h in range(2):
            differ(0, cols(h))
        differ(1, whole)
        hidden(2, "b6")
        hidden(3, "b7")
        differ(2, whole)
        bias_cols = ps.tile([P, P], F32, name="bias_cols", tag="b3")
        nc.tensor.transpose(bias_cols[:], bias_rows[:], ident[:])
        nc.vector.tensor_scalar(
            out=half_bias[:], in0=bias_cols[:, 0:4], scalar1=-0.5, scalar2=zero[:], op0=ALU.mult, op1=ALU.add
        )
        gate(0, "b4")
        gate(1, "b5")
        gate(2, "b0")
        gate(3, "b1")
        weigh(0, whole, sb.tile([P, J], F32, name="part0")[:])
        for c, h in ((1, 1), (1, 0), (2, 0), (2, 1)):
            weigh(c, cols(h), sb.tile([P, HALF], F32, name="part%d%d" % (c, h))[:])
        sum_close(0, sum_open(0, 4, "b4"))
        sum_close(1, sum_open(1, 2, "b5"))
        turn_back(0, 4, "b2")
        turn_back(1, 2, "b6")
        finish(1, cols(1))
        store(1, cols(1))
        for h in range(2):
            finish(2, cols(h))
        store(2, whole)
        for h in range(2):
            differ(3, cols(h))
        for h in range(2):
            weigh(3, cols(h), sb.tile([P, HALF], F32, name="part3%d" % h)[:])
        for h in range(2):
            finish(3, cols(h))
            store(3, cols(h))
